import numpy as np
import ml_dtypes


def mxq(x, axis, fmt="e4m3"):
    dtype, down = {"e4m3": (ml_dtypes.float8_e4m3fn, 7), "e5m2": (ml_dtypes.float8_e5m2, 14)}[fmt]
    v = np.moveaxis(np.asarray(x, np.float32).astype(ml_dtypes.bfloat16).astype(np.float64), axis, -1)
    blocks = v.reshape(v.shape[:-1] + (-1, 32))
    amax = np.abs(blocks).max(-1, keepdims=True)
    byte = np.maximum(np.where(amax > 0, np.frexp(amax)[1] - 1 + 127, 0) - down, 1)
    scale = np.exp2(byte - 127.0)
    codes = (blocks / scale).astype(np.float32).astype(dtype).astype(np.float64)
    return np.moveaxis((codes * scale).reshape(v.shape), -1, axis)


WIDE = False


def mx_kscale(k):
    if not WIDE:
        return np.ones(k)
    levels = np.array([24, -24, 12, -12, 0])
    if k % 512:
        return np.exp2(np.random.permutation(np.resize(levels, k // 32))).repeat(32)
    a = np.empty((k // 512, 16))
    for p in range(k // 512):
        a[p, :8] = np.random.permutation(np.resize(levels, 8))
        for g in range(8):
            far = levels[np.abs(levels - a[p, g]) >= 10]
            a[p, g + 8] = far[np.random.randint(len(far))]
    return np.exp2(a.ravel()).repeat(32)


def f64(x):
    return np.asarray(x).astype(np.float64)


def striped(idx):
    return np.tile(idx.reshape(-1, 16).T, (8, 1)).astype(np.uint16)


def unstriped(offs):
    return offs[:16].T.reshape(-1).astype(np.int64)


E2M1 = np.array([0.0, 0.5, 1.0, 1.5, 2.0, 3.0, 4.0, 6.0, -0.0, -0.5, -1.0, -1.5, -2.0, -3.0, -4.0, -6.0])


def pack_weight(w, fmt):
    k, n = w.shape
    w = f64(np.asarray(w, np.float32).astype(ml_dtypes.bfloat16)).reshape(k // 32, 32, n)
    amax = np.abs(w).max(1)
    if fmt == "e4m3":
        byte = np.frexp(amax)[1] - 1 + 127 - 7
    else:
        mant, ex = np.frexp(amax / 6.0)
        byte = np.where(mant > 0.5, ex, ex - 1) + 127
    byte = np.clip(np.where(amax > 0, byte, 1), 1, 254)
    scaled = (w * np.exp2(127.0 - byte)[:, None, :]).reshape(k, n).astype(np.float32)
    by_word = np.ascontiguousarray(scaled.reshape(k // 512, 128, 4, n).transpose(0, 1, 3, 2))
    if fmt == "e4m3":
        words = by_word.astype(ml_dtypes.float8_e4m3fn).view(np.uint8)
    else:
        c = by_word.astype(ml_dtypes.float4_e2m1fn).view(np.uint8) & 0xF
        words = (c[..., 0::2] | (c[..., 1::2] << 4)).reshape(k // 512, 128, 2 * n)
    return np.ascontiguousarray(words), np.ascontiguousarray(byte.astype(np.uint8).reshape(k // 512, 16, n))


def unpack_weight(words, scales, fmt):
    g, _, n = scales.shape
    words = np.ascontiguousarray(words).reshape(g, 128, n, -1)
    if fmt == "e4m3":
        vals = words.view(ml_dtypes.float8_e4m3fn).astype(np.float64)
    else:
        nib = np.empty((g, 128, n, 4), np.uint8)
        nib[..., 0::2] = words & 0xF
        nib[..., 1::2] = words >> 4
        vals = E2M1[nib]
    vals = vals * np.repeat(np.exp2(scales.astype(np.float64) - 127.0), 8, axis=1)[..., None]
    return vals.transpose(0, 1, 3, 2).reshape(g * 512, n)


def pack_table4(v):
    words, scales = pack_weight(v, "e2m1")
    g, t = words.shape[0] // 2, v.shape[1]
    return np.ascontiguousarray(words.reshape(g, 2, 128, t, 2).transpose(0, 2, 3, 1, 4).reshape(g, 128, t, 4)), scales


def unpack_table4(words, scales):
    g, _, t, _ = words.shape
    return unpack_weight(words.reshape(g, 128, t, 2, 2).transpose(0, 3, 1, 2, 4).reshape(2 * g, 128, 2 * t), scales, "e2m1")


K, R, N, T, J = 1024, 512, 256, 4096, 512


def setup_inputs():
    n = np.random.standard_normal
    s = mx_kscale(K)[:, None]
    u = mx_kscale(R)[:, None]
    p_tab = pack_table4(n((K, T)) * s)
    p_wc = pack_weight(n((K, R)) / np.sqrt(K) / s * u.T, "e2m1")
    return {
        "tab_words": p_tab[0],
        "tab_scales": p_tab[1],
        "c": (n((K, J)) * s).astype(np.float32),
        "w": (n((K, R)) / np.sqrt(K) / s * u.T).astype(np.float32),
        "wc_words": p_wc[0],
        "wc_scales": p_wc[1],
        "wd": (n((R, N)) / np.sqrt(R) / u).astype(np.float32),
        "res": (n((N, J))).astype(np.float32),
        "offs": striped(np.concatenate([np.random.permutation(T)[:J] for _ in range(2)])),
    }


def reference(tab_words, tab_scales, c, w, wc_words, wc_scales, wd, res, offs):
    idx = unstriped(offs).reshape(2, J)
    tab_ = unpack_table4(tab_words, tab_scales)[:, idx]
    c_ = mxq(f64(c), 0, "e4m3")
    w_ = mxq(f64(w), 0, "e4m3")
    a0 = w_.T @ tab_[:, 0]
    a1 = w_.T @ tab_[:, 1]
    wc_ = unpack_weight(wc_words, wc_scales, "e2m1")
    ac = wc_.T @ c_
    h = np.maximum(np.maximum(a0, a1) + ac, 0.0)
    h_ = mxq(h, 0, "e4m3")
    wd_ = mxq(f64(wd), 0, "e4m3")
    y = wd_.T @ h_
    return f64(res) + y

@@ -1,0 +1,211 @@
+from contextlib import ExitStack
+
+import concourse.mybir as mybir
+
+K, R, N, T, J = 1024, 512, 256, 4096, 512
+FLOPS = 2 * K * R * J * 3 + 2 * R * N * J
+
+F32 = mybir.dt.float32
+BF16 = mybir.dt.bfloat16
+I32 = mybir.dt.int32
+U32 = mybir.dt.uint32
+U16 = mybir.dt.uint16
+U8 = mybir.dt.uint8
+FP8X4 = mybir.dt.float8_e4m3fn_x4
+FP4X4 = mybir.dt.float4_e2m1fn_x4
+ALU = mybir.AluOpType
+
+P = 128
+JB = 128
+
+
+def tile_list_pnet_res_kernel(
+    tc, tab_words, tab_scales, c, w, wc_words, wc_scales, wd, res, offs, out
+):
+    nc = tc.nc
+    with ExitStack() as ctx:
+        sb = ctx.enter_context(tc.tile_pool(name="sb", bufs=1))
+        ps = ctx.enter_context(tc.psum_pool(name="ps", bufs=1))
+
+        def tile(shape, dtype, name):
+            return sb.tile(shape, dtype, name=name, align_bytes=64)
+
+        offsets = sb.tile([P, 2 * J // 16], U16, name="offsets")
+        nc.sync.dma_start(offsets[:], offs)
+        swin = sb.tile([P, T], U8, name="swin", tag="shared", align_bytes=64)
+        nc.sync.dma_start(swin[0:32, :].bitcast(I32), tab_scales.rearrange("a q t -> (a q) t").bitcast(I32))
+        twin = tile([P, T], I32, "twin")
+        nc.sync.dma_start(twin[:], tab_words[0].rearrange("p t b -> p (t b)").bitcast(I32))
+        w0_raw = tile([P, 4 * R], F32, "w0_raw")
+        nc.sync.dma_start(w0_raw[:], w[0:512, :].rearrange("(p i) r -> p (i r)", i=4))
+        wcw_raw = tile([P, 2, R // 2], I32, "wcw_raw")
+        nc.sync.dma_start(wcw_raw[:], wc_words.rearrange("a p b -> p a b").bitcast(I32))
+
+        nc.vector.memset(swin[32:64, :].bitcast(I32), 0)
+        nc.vector.memset(swin[64:128, :].bitcast(I32), 0)
+        wcs_raw = tile([P, 2, R], U8, "wcs_raw")
+        nc.vector.memset(wcs_raw[:].rearrange("p a r -> p (a r)").bitcast(I32), 0)
+        tplane = [tile([P, 2 * J], U8, "tplane%d" % a) for a in range(2)]
+        for a in range(2):
+            nc.vector.memset(tplane[a][:].bitcast(I32), 0)
+        for q in range(4):
+            nc.scalar.dma_start(
+                wcs_raw[32 * q : 32 * q + 4, :, :].bitcast(I32),
+                wc_scales[:, 4 * q : 4 * q + 4, :].rearrange("a s r -> s a r").bitcast(I32),
+            )
+
+        sgot = tile([P, 2 * J], U8, "sgot")
+        nc.vector.tensor_copy(sgot[:], swin[:].indirect(offsets[:]))
+
+        def move_plane(a):
+            for q in range(4):
+                nc.sync.dma_start(
+                    tplane[a][32 * q : 32 * q + 4, :].bitcast(I32),
+                    sgot[16 * a + 4 * q : 16 * a + 4 * q + 4, :].bitcast(I32),
+                )
+
+        late = sb.tile([P, 8192], F32, name="late", tag="shared", align_bytes=64)
+        move_plane(0)
+        w1_raw = late[:, 0:2048]
+        nc.sync.dma_start(w1_raw, w[512:1024, :].rearrange("(p i) r -> p (i r)", i=4))
+        move_plane(1)
+        w_raw = [w0_raw[:], w1_raw]
+        nc.sync.dma_start(late[:, 2048:4096], c[0:512, :].rearrange("(p i) j -> p (i j)", i=4))
+        c0_raw = late[:, 2048:4096].rearrange("p (i j) -> p i j", i=4)
+        c1_raw = [late[:, 4096 + 1024 * hf : 4096 + 1024 * (hf + 1)].rearrange("p (i j) -> p i j", i=4) for hf in range(2)]
+        for hf in range(2):
+            nc.sync.dma_start(c1_raw[hf], c[512:1024, 256 * hf : 256 * (hf + 1)].rearrange("(p i) j -> p i j", i=4))
+        wd_raw = late[:, 6144:7168].rearrange("p (i j) -> p i j", i=4)
+        wd_v = wd.rearrange("(b t e) n -> t b e n", t=4, e=8)
+        for t in range(4):
+            nc.sync.dma_start(wd_raw[:, t, :], wd_v[t])
+        res_sb = late[:, 7168:8192].rearrange("p (h j) -> p h j", h=2)
+        nc.sync.dma_start(res_sb, res.rearrange("(h p) j -> p h j", h=2))
+
+        tgot = tile([P, 2 * J], U32, "tgot")
+        nc.vector.tensor_copy(tgot[:], twin[:].bitcast(U32).indirect(offsets[:]))
+        tcodes = tile([P, 2, 4 * J], U8, "tcodes")
+        nc.vector.tensor_copy(tcodes[:].bitcast(U16), tgot[:].bitcast(U16).rearrange("p (j d) -> p d j", d=2))
+
+        w_codes = [tile([P, R], U32, "w_codes%d" % a) for a in range(2)]
+        w_sc = [tile([P, R], U8, "w_sc%d" % a) for a in range(2)]
+        for a in range(2):
+            wg = tile([P, 4 * R], BF16, "wg%d" % a)
+            nc.scalar.copy(
+                wg[:].rearrange("p (t b e i) -> p t b i e", t=4, e=8, i=4),
+                w_raw[a].rearrange("p (i b t e) -> p t b i e", i=4, t=4, e=8),
+            )
+            nc.vector.quantize_mx(w_codes[a][:].bitcast(FP8X4), w_sc[a][:], wg[:])
+
+        nb = [ [ps.tile([P, 4, JB], F32, name="nb%d_%d" % (g, b), tag="bank%d" % (4 * g + b)) for b in range(4)] for g in range(2)]
+        for a in range(2):
+            for b in range(4):
+                for g in range(2):
+                    cols = slice(J * g + JB * b, J * g + JB * (b + 1))
+                    for t in range(4):
+                        nc.tensor.matmul_mx(
+                            nb[g][b][:, t, :],
+                            lhsT=w_codes[a][:, P * t : P * (t + 1)].bitcast(FP8X4),
+                            lhsT_scale=w_sc[a][:, P * t : P * (t + 1)],
+                            rhs=tcodes[:, a, 2 * cols.start : 2 * cols.stop].bitcast(FP4X4),
+                            rhs_scale=tplane[a][:, cols],
+                            start=(a == 0 and t == 0),
+                            stop=(a == 1 and t == 3),
+                        )
+
+        wc_codes = tile([P, 2, 2 * R], U8, "wc_codes")
+        nc.vector.tensor_copy(
+            wc_codes[:].bitcast(I32).rearrange("p a (t b e) -> p a t b e", t=4, e=4),
+            wcw_raw[:].rearrange("p a (b t e) -> p a t b e", t=4, e=4),
+        )
+        wc_sc = tile([P, 2, R], U8, "wc_sc")
+        nc.vector.tensor_copy(
+            wc_sc[:].bitcast(I32).rearrange("p a (t b e) -> p a t b e", t=4, e=2),
+            wcs_raw[:].bitcast(I32).rearrange("p a (b t e) -> p a t b e", t=4, e=2),
+        )
+
+        def cast_c(raw, width, name):
+            g = tile([P, 4 * width], BF16, name)
+            nc.scalar.copy(
+                g[:].rearrange("p (u v i) -> p u i v", v=4, i=4),
+                raw.rearrange("p i (u v) -> p u i v", v=4),
+            )
+            return g
+
+        c_codes = [[tile([P, J // 2], U32, "c_codes%d_%d" % (a, hf)) for hf in range(2)] for a in range(2)]
+        c_sc = [[tile([P, J // 2], U8, "c_sc%d_%d" % (a, hf)) for hf in range(2)] for a in range(2)]
+
+        def quant_c(a, hf, raw):
+            g = cast_c(raw, J // 2, "cg%d_%d" % (a, hf))
+            nc.vector.quantize_mx(c_codes[a][hf][:].bitcast(FP8X4), c_sc[a][hf][:], g[:])
+
+        pooled = [tile([P, 4 * JB], F32, "pooled%d" % b) for b in range(4)]
+
+        def pool_max(b):
+            first = tile([P, 4 * JB], F32, "first%d" % b)
+            nc.scalar.copy(first[:].rearrange("p (j t) -> p j t", t=4), nb[0][b][:].rearrange("p t j -> p j t"))
+            nc.vector.tensor_tensor(
+                pooled[b][:].rearrange("p (j t) -> p j t", t=4),
+                nb[1][b][:].rearrange("p t j -> p j t"),
+                first[:].rearrange("p (j t) -> p j t", t=4),
+                ALU.max,
+            )
+
+        quant_c(0, 0, c0_raw[:, :, 0:256])
+        pool_max(0)
+        pool_max(1)
+        quant_c(1, 0, c1_raw[0])
+        quant_c(0, 1, c0_raw[:, :, 256:512])
+        pool_max(2)
+        pool_max(3)
+        quant_c(1, 1, c1_raw[1])
+
+        wdg = tile([P, 4 * N], BF16, "wdg")
+        nc.scalar.copy(
+            wdg[:].rearrange("p (u v i) -> p u i v", v=4, i=4), wd_raw.rearrange("p i (u v) -> p u i v", v=4)
+        )
+        wd_codes = tile([P, N], U32, "wd_codes")
+        wd_sc = tile([P, N], U8, "wd_sc")
+        nc.vector.quantize_mx(wd_codes[:].bitcast(FP8X4), wd_sc[:], wdg[:])
+
+        for hf in range(2):
+            hb = tile([P, 4 * 2 * JB], BF16, "hb%d" % hf)
+            for bb in range(2):
+                b = 2 * hf + bb
+                own = ps.tile([P, 4, JB], F32, name="own%d" % b, tag="bank%d" % b)
+                for a in range(2):
+                    for t in range(4):
+                        nc.tensor.matmul_mx(
+                            own[:, t, :],
+                            lhsT=wc_codes[:, a, 2 * P * t : 2 * P * (t + 1)].bitcast(FP4X4),
+                            lhsT_scale=wc_sc[:, a, P * t : P * (t + 1)],
+                            rhs=c_codes[a][hf][:, JB * bb : JB * (bb + 1)].bitcast(FP8X4),
+                            rhs_scale=c_sc[a][hf][:, JB * bb : JB * (bb + 1)],
+                            start=(a == 0 and t == 0),
+                            stop=(a == 1 and t == 3),
+                        )
+                nc.vector.tensor_tensor(
+                    hb[:, 512 * bb : 512 * (bb + 1)].rearrange("p (j t) -> p j t", t=4),
+                    own[:].rearrange("p t j -> p j t"),
+                    pooled[b][:].rearrange("p (j t) -> p j t", t=4),
+                    ALU.add,
+                )
+            hr = tile([P, 4 * 2 * JB], BF16, "hr%d" % hf)
+            nc.vector.tensor_scalar_max(hr[:], hb[:], 0.0)
+            h_codes = tile([P, 2 * JB], U32, "h_codes%d" % hf)
+            h_sc = tile([P, 2 * JB], U8, "h_sc%d" % hf)
+            nc.vector.quantize_mx(h_codes[:].bitcast(FP8X4), h_sc[:], hr[:])
+            y = ps.tile([P, 2, 2 * JB], F32, name="y%d" % hf, tag="bank%d" % (4 + hf))
+            for nh in range(2):
+                nc.tensor.matmul_mx(
+                    y[:, nh, :],
+                    lhsT=wd_codes[:, P * nh : P * (nh + 1)].bitcast(FP8X4),
+                    lhsT_scale=wd_sc[:, P * nh : P * (nh + 1)],
+                    rhs=h_codes[:].bitcast(FP8X4),
+                    rhs_scale=h_sc[:],
+                    start=True,
+                    stop=True,
+                )
+            o = tile([P, 2, 2 * JB], F32, "o%d" % hf)
+            nc.vector.tensor_tensor(o[:], y[:], res_sb[:, :, 256 * hf : 256 * (hf + 1)], ALU.add)
+            nc.sync.dma_start(out.rearrange("(h p) j -> p h j", h=2)[:, :, 256 * hf : 256 * (hf + 1)], o[:])

@@ -34,17 +34,17 @@ def tile_list_pnet_res_kernel(
         nc.sync.dma_start(offsets[:], offs)
         swin = sb.tile([P, T], U8, name="swin", tag="shared", align_bytes=64)
         nc.sync.dma_start(swin[0:32, :].bitcast(I32), tab_scales.rearrange("a q t -> (a q) t").bitcast(I32))
+        wcw_raw = tile([P, 2, R // 2], I32, "wcw_raw")
+        nc.sync.dma_start(wcw_raw[:], wc_words.rearrange("a p b -> p a b").bitcast(I32))
         twin = tile([P, T], I32, "twin")
         nc.sync.dma_start(twin[:], tab_words[0].rearrange("p t b -> p (t b)").bitcast(I32))
         w0_raw = tile([P, 4 * R], F32, "w0_raw")
         nc.sync.dma_start(w0_raw[:], w[0:512, :].rearrange("(p i) r -> p (i r)", i=4))
-        wcw_raw = tile([P, 2, R // 2], I32, "wcw_raw")
-        nc.sync.dma_start(wcw_raw[:], wc_words.rearrange("a p b -> p a b").bitcast(I32))
 
-        nc.vector.memset(swin[32:64, :].bitcast(I32), 0)
-        nc.vector.memset(swin[64:128, :].bitcast(I32), 0)
         wcs_raw = tile([P, 2, R], U8, "wcs_raw")
         nc.vector.memset(wcs_raw[:].rearrange("p a r -> p (a r)").bitcast(I32), 0)
+        nc.vector.memset(swin[32:64, :].bitcast(I32), 0)
+        nc.vector.memset(swin[64:128, :].bitcast(I32), 0)
         tplane = [tile([P, 2 * J], U8, "tplane%d" % a) for a in range(2)]
         for a in range(2):
             nc.vector.memset(tplane[a][:].bitcast(I32), 0)
@@ -57,18 +57,18 @@ def tile_list_pnet_res_kernel(
         sgot = tile([P, 2 * J], U8, "sgot")
         nc.vector.tensor_copy(sgot[:], swin[:].indirect(offsets[:]))
 
-        def move_plane(a):
+        def move_plane(a, queue):
             for q in range(4):
-                nc.sync.dma_start(
+                queue.dma_start(
                     tplane[a][32 * q : 32 * q + 4, :].bitcast(I32),
                     sgot[16 * a + 4 * q : 16 * a + 4 * q + 4, :].bitcast(I32),
                 )
 
         late = sb.tile([P, 8192], F32, name="late", tag="shared", align_bytes=64)
-        move_plane(0)
+        move_plane(0, nc.sync)
         w1_raw = late[:, 0:2048]
         nc.sync.dma_start(w1_raw, w[512:1024, :].rearrange("(p i) r -> p (i r)", i=4))
-        move_plane(1)
+        move_plane(1, nc.sync)
         w_raw = [w0_raw[:], w1_raw]
         nc.sync.dma_start(late[:, 2048:4096], c[0:512, :].rearrange("(p i) j -> p (i j)", i=4))
         c0_raw = late[:, 2048:4096].rearrange("p (i j) -> p i j", i=4)
@@ -76,57 +76,70 @@ def tile_list_pnet_res_kernel(
         for hf in range(2):
             nc.sync.dma_start(c1_raw[hf], c[512:1024, 256 * hf : 256 * (hf + 1)].rearrange("(p i) j -> p i j", i=4))
         wd_raw = late[:, 6144:7168].rearrange("p (i j) -> p i j", i=4)
-        wd_v = wd.rearrange("(b t e) n -> t b e n", t=4, e=8)
+        wd_v = wd.rearrange("(b t e) n -> t b e n", t=4, e=4)
         for t in range(4):
             nc.sync.dma_start(wd_raw[:, t, :], wd_v[t])
         res_sb = late[:, 7168:8192].rearrange("p (h j) -> p h j", h=2)
         nc.sync.dma_start(res_sb, res.rearrange("(h p) j -> p h j", h=2))
+
+        wc_codes = tile([P, 2, 2 * R], U8, "wc_codes")
+        nc.vector.tensor_copy(
+            wc_codes[:].bitcast(I32).rearrange("p a (t b e) -> p a t b e", t=4, e=2),
+            wcw_raw[:].rearrange("p a (b t e) -> p a t b e", t=4, e=2),
+        )
+        wc_sc = tile([P, 2, R], U8, "wc_sc")
+        nc.vector.tensor_copy(
+            wc_sc[:].bitcast(I32).rearrange("p a (t b) -> p a t b", t=4),
+            wcs_raw[:].bitcast(I32).rearrange("p a (b t) -> p a t b", t=4),
+        )
 
         tgot = tile([P, 2 * J], U32, "tgot")
         nc.vector.tensor_copy(tgot[:], twin[:].bitcast(U32).indirect(offsets[:]))
         tcodes = tile([P, 2, 4 * J], U8, "tcodes")
         nc.vector.tensor_copy(tcodes[:].bitcast(U16), tgot[:].bitcast(U16).rearrange("p (j d) -> p d j", d=2))
 
-        w_codes = [tile([P, R], U32, "w_codes%d" % a) for a in range(2)]
-        w_sc = [tile([P, R], U8, "w_sc%d" % a) for a in range(2)]
-        for a in range(2):
-            wg = tile([P, 4 * R], BF16, "wg%d" % a)
-            nc.scalar.copy(
-                wg[:].rearrange("p (t b e i) -> p t b i e", t=4, e=8, i=4),
-                w_raw[a].rearrange("p (i b t e) -> p t b i e", i=4, t=4, e=8),
+        w_codes = [[tile([P, 2 * P], U32, "w_codes%d_%d" % (a, u)) for u in range(2)] for a in range(2)]
+        w_sc = [[tile([P, 2 * P], U8, "w_sc%d_%d" % (a, u)) for u in range(2)] for a in range(2)]
+        wg = [[tile([P, 8 * P], BF16, "wg%d_%d" % (a, u)) for u in range(2)] for a in range(2)]
+
+        def cast_w(a, u, copy):
+            copy(
+                wg[a][u][:].rearrange("p (t b e i) -> p t b i e", t=2, e=4, i=4),
+                w_raw[a].rearrange("p (i b t e) -> p t b i e", i=4, t=4, e=4)[:, 2 * u : 2 * u + 2],
             )
-            nc.vector.quantize_mx(w_codes[a][:].bitcast(FP8X4), w_sc[a][:], wg[:])
+
+        def quant_w(a, u):
+            nc.vector.quantize_mx(w_codes[a][u][:].bitcast(FP8X4), w_sc[a][u][:], wg[a][u][:])
+
+        cast_w(0, 0, nc.scalar.copy)
+        cast_w(0, 1, nc.scalar.copy)
+        quant_w(0, 0)
+        quant_w(0, 1)
+        cast_w(1, 0, nc.scalar.copy)
+        cast_w(1, 1, nc.vector.tensor_copy)
+        quant_w(1, 0)
+        quant_w(1, 1)
 
         nb = [ [ps.tile([P, 4, JB], F32, name="nb%d_%d" % (g, b), tag="bank%d" % (4 * g + b)) for b in range(4)] for g in range(2)]
-        for a in range(2):
-            for b in range(4):
+        for b in range(4):
+            for a in range(2):
                 for g in range(2):
                     cols = slice(J * g + JB * b, J * g + JB * (b + 1))
                     for t in range(4):
+                        wcols = slice(P * (t % 2), P * (t % 2 + 1))
                         nc.tensor.matmul_mx(
                             nb[g][b][:, t, :],
-                            lhsT=w_codes[a][:, P * t : P * (t + 1)].bitcast(FP8X4),
-                            lhsT_scale=w_sc[a][:, P * t : P * (t + 1)],
+                            lhsT=w_codes[a][t // 2][:, wcols].bitcast(FP8X4),
+                            lhsT_scale=w_sc[a][t // 2][:, wcols],
                             rhs=tcodes[:, a, 2 * cols.start : 2 * cols.stop].bitcast(FP4X4),
                             rhs_scale=tplane[a][:, cols],
                             start=(a == 0 and t == 0),
                             stop=(a == 1 and t == 3),
                         )
 
-        wc_codes = tile([P, 2, 2 * R], U8, "wc_codes")
-        nc.vector.tensor_copy(
-            wc_codes[:].bitcast(I32).rearrange("p a (t b e) -> p a t b e", t=4, e=4),
-            wcw_raw[:].rearrange("p a (b t e) -> p a t b e", t=4, e=4),
-        )
-        wc_sc = tile([P, 2, R], U8, "wc_sc")
-        nc.vector.tensor_copy(
-            wc_sc[:].bitcast(I32).rearrange("p a (t b e) -> p a t b e", t=4, e=2),
-            wcs_raw[:].bitcast(I32).rearrange("p a (b t e) -> p a t b e", t=4, e=2),
-        )
-
-        def cast_c(raw, width, name):
+        def interleave(raw, width, name, copy):
             g = tile([P, 4 * width], BF16, name)
-            nc.scalar.copy(
+            copy(
                 g[:].rearrange("p (u v i) -> p u i v", v=4, i=4),
                 raw.rearrange("p i (u v) -> p u i v", v=4),
             )
@@ -135,8 +148,7 @@ def tile_list_pnet_res_kernel(
         c_codes = [[tile([P, J // 2], U32, "c_codes%d_%d" % (a, hf)) for hf in range(2)] for a in range(2)]
         c_sc = [[tile([P, J // 2], U8, "c_sc%d_%d" % (a, hf)) for hf in range(2)] for a in range(2)]
 
-        def quant_c(a, hf, raw):
-            g = cast_c(raw, J // 2, "cg%d_%d" % (a, hf))
+        def quant_c(a, hf, g):
             nc.vector.quantize_mx(c_codes[a][hf][:].bitcast(FP8X4), c_sc[a][hf][:], g[:])
 
         pooled = [tile([P, 4 * JB], F32, "pooled%d" % b) for b in range(4)]
@@ -151,50 +163,52 @@ def tile_list_pnet_res_kernel(
                 ALU.max,
             )
 
-        quant_c(0, 0, c0_raw[:, :, 0:256])
+        g00 = interleave(c0_raw[:, :, 0:256], 256, "cg00", nc.scalar.copy)
+        g01 = interleave(c0_raw[:, :, 256:512], 256, "cg01", nc.vector.tensor_copy)
+        quant_c(0, 0, g00)
+        quant_c(0, 1, g01)
         pool_max(0)
+        quant_c(1, 0, interleave(c1_raw[0], 256, "cg10", nc.scalar.copy))
         pool_max(1)
-        quant_c(1, 0, c1_raw[0])
-        quant_c(0, 1, c0_raw[:, :, 256:512])
         pool_max(2)
         pool_max(3)
-        quant_c(1, 1, c1_raw[1])
+        quant_c(1, 1, interleave(c1_raw[1], 256, "cg11", nc.vector.tensor_copy))
+        wdg = interleave(wd_raw, N, "wdg", nc.scalar.copy)
 
-        wdg = tile([P, 4 * N], BF16, "wdg")
-        nc.scalar.copy(
-            wdg[:].rearrange("p (u v i) -> p u i v", v=4, i=4), wd_raw.rearrange("p i (u v) -> p u i v", v=4)
-        )
+        hb = [tile([P, 8 * JB], BF16, "hb%d" % hf) for hf in range(2)]
+        hr = [tile([P, 8 * JB], BF16, "hr%d" % hf) for hf in range(2)]
         wd_codes = tile([P, N], U32, "wd_codes")
         wd_sc = tile([P, N], U8, "wd_sc")
-        nc.vector.quantize_mx(wd_codes[:].bitcast(FP8X4), wd_sc[:], wdg[:])
+        ys = [None, None]
 
-        for hf in range(2):
-            hb = tile([P, 4 * 2 * JB], BF16, "hb%d" % hf)
-            for bb in range(2):
-                b = 2 * hf + bb
-                own = ps.tile([P, 4, JB], F32, name="own%d" % b, tag="bank%d" % b)
-                for a in range(2):
-                    for t in range(4):
-                        nc.tensor.matmul_mx(
-                            own[:, t, :],
-                            lhsT=wc_codes[:, a, 2 * P * t : 2 * P * (t + 1)].bitcast(FP4X4),
-                            lhsT_scale=wc_sc[:, a, P * t : P * (t + 1)],
-                            rhs=c_codes[a][hf][:, JB * bb : JB * (bb + 1)].bitcast(FP8X4),
-                            rhs_scale=c_sc[a][hf][:, JB * bb : JB * (bb + 1)],
-                            start=(a == 0 and t == 0),
-                            stop=(a == 1 and t == 3),
-                        )
-                nc.vector.tensor_tensor(
-                    hb[:, 512 * bb : 512 * (bb + 1)].rearrange("p (j t) -> p j t", t=4),
-                    own[:].rearrange("p t j -> p j t"),
-                    pooled[b][:].rearrange("p (j t) -> p j t", t=4),
-                    ALU.add,
-                )
-            hr = tile([P, 4 * 2 * JB], BF16, "hr%d" % hf)
-            nc.vector.tensor_scalar_max(hr[:], hb[:], 0.0)
+        def own_add(b):
+            hf, bb = divmod(b, 2)
+            own = ps.tile([P, 4, JB], F32, name="own%d" % b, tag="bank%d" % b)
+            for a in range(2):
+                for t in range(4):
+                    nc.tensor.matmul_mx(
+                        own[:, t, :],
+                        lhsT=wc_codes[:, a, 2 * P * t : 2 * P * (t + 1)].bitcast(FP4X4),
+                        lhsT_scale=wc_sc[:, a, P * t : P * (t + 1)],
+                        rhs=c_codes[a][hf][:, JB * bb : JB * (bb + 1)].bitcast(FP8X4),
+                        rhs_scale=c_sc[a][hf][:, JB * bb : JB * (bb + 1)],
+                        start=(a == 0 and t == 0),
+                        stop=(a == 1 and t == 3),
+                    )
+            nc.vector.tensor_tensor(
+                hb[hf][:, 512 * bb : 512 * (bb + 1)].rearrange("p (j t) -> p j t", t=4),
+                own[:].rearrange("p t j -> p j t"),
+                pooled[b][:].rearrange("p (j t) -> p j t", t=4),
+                ALU.add,
+            )
+
+        def relu(hf):
+            nc.vector.tensor_scalar_max(hr[hf][:], hb[hf][:], 0.0)
+
+        def second(hf):
             h_codes = tile([P, 2 * JB], U32, "h_codes%d" % hf)
             h_sc = tile([P, 2 * JB], U8, "h_sc%d" % hf)
-            nc.vector.quantize_mx(h_codes[:].bitcast(FP8X4), h_sc[:], hr[:])
+            nc.vector.quantize_mx(h_codes[:].bitcast(FP8X4), h_sc[:], hr[hf][:])
             y = ps.tile([P, 2, 2 * JB], F32, name="y%d" % hf, tag="bank%d" % (4 + hf))
             for nh in range(2):
                 nc.tensor.matmul_mx(
@@ -206,6 +220,21 @@ def tile_list_pnet_res_kernel(
                     start=True,
                     stop=True,
                 )
+            return y
+
+        def finish(hf, y):
             o = tile([P, 2, 2 * JB], F32, "o%d" % hf)
             nc.vector.tensor_tensor(o[:], y[:], res_sb[:, :, 256 * hf : 256 * (hf + 1)], ALU.add)
             nc.sync.dma_start(out.rearrange("(h p) j -> p h j", h=2)[:, :, 256 * hf : 256 * (hf + 1)], o[:])
+
+        own_add(0)
+        own_add(1)
+        relu(0)
+        own_add(2)
+        own_add(3)
+        nc.vector.quantize_mx(wd_codes[:].bitcast(FP8X4), wd_sc[:], wdg[:])
+        y0 = second(0)
+        relu(1)
+        finish(0, y0)
+        y1 = second(1)
+        finish(1, y1)

@@ -34,9 +34,7 @@ def tile_list_pnet_res_kernel(
         nc.sync.dma_start(offsets[:], offs)
         swin = sb.tile([P, T], U8, name="swin", tag="shared", align_bytes=64)
         nc.sync.dma_start(swin[0:32, :].bitcast(I32), tab_scales.rearrange("a q t -> (a q) t").bitcast(I32))
-        wcw_raw = tile([P, 2, R // 2], I32, "wcw_raw")
-        nc.sync.dma_start(wcw_raw[:], wc_words.rearrange("a p b -> p a b").bitcast(I32))
-        twin = tile([P, T], I32, "twin")
+        twin = sb.tile([P, T], I32, name="twin", tag="words", align_bytes=64)
         nc.sync.dma_start(twin[:], tab_words[0].rearrange("p t b -> p (t b)").bitcast(I32))
         w0_raw = tile([P, 4 * R], F32, "w0_raw")
         nc.sync.dma_start(w0_raw[:], w[0:512, :].rearrange("(p i) r -> p (i r)", i=4))
@@ -57,6 +55,11 @@ def tile_list_pnet_res_kernel(
         sgot = tile([P, 2 * J], U8, "sgot")
         nc.vector.tensor_copy(sgot[:], swin[:].indirect(offsets[:]))
 
+        tgot = sb.tile([P, 2 * J], U32, name="tgot", tag="got", align_bytes=64)
+        nc.vector.tensor_copy(tgot[:], twin[:].bitcast(U32).indirect(offsets[:]))
+        tcodes = tile([P, 2, 4 * J], U8, "tcodes")
+        nc.vector.tensor_copy(tcodes[:].bitcast(U16), tgot[:].bitcast(U16).rearrange("p (j d) -> p d j", d=2))
+
         def move_plane(a, queue):
             for q in range(4):
                 queue.dma_start(
@@ -73,30 +76,16 @@ def tile_list_pnet_res_kernel(
         nc.sync.dma_start(late[:, 2048:4096], c[0:512, :].rearrange("(p i) j -> p (i j)", i=4))
         c0_raw = late[:, 2048:4096].rearrange("p (i j) -> p i j", i=4)
         c1_raw = [late[:, 4096 + 1024 * hf : 4096 + 1024 * (hf + 1)].rearrange("p (i j) -> p i j", i=4) for hf in range(2)]
-        for hf in range(2):
-            nc.sync.dma_start(c1_raw[hf], c[512:1024, 256 * hf : 256 * (hf + 1)].rearrange("(p i) j -> p i j", i=4))
+        nc.sync.dma_start(c1_raw[0], c[512:1024, 0:256].rearrange("(p i) j -> p i j", i=4))
+        wcw_raw = sb.tile([P, 2, R // 2], I32, name="wcw_raw", tag="words", align_bytes=64)
+        nc.sync.dma_start(wcw_raw[:], wc_words.rearrange("a p b -> p a b").bitcast(I32))
+        nc.sync.dma_start(c1_raw[1], c[512:1024, 256:512].rearrange("(p i) j -> p i j", i=4))
         wd_raw = late[:, 6144:7168].rearrange("p (i j) -> p i j", i=4)
         wd_v = wd.rearrange("(b t e) n -> t b e n", t=4, e=4)
         for t in range(4):
             nc.sync.dma_start(wd_raw[:, t, :], wd_v[t])
         res_sb = late[:, 7168:8192].rearrange("p (h j) -> p h j", h=2)
         nc.sync.dma_start(res_sb, res.rearrange("(h p) j -> p h j", h=2))
-
-        wc_codes = tile([P, 2, 2 * R], U8, "wc_codes")
-        nc.vector.tensor_copy(
-            wc_codes[:].bitcast(I32).rearrange("p a (t b e) -> p a t b e", t=4, e=2),
-            wcw_raw[:].rearrange("p a (b t e) -> p a t b e", t=4, e=2),
-        )
-        wc_sc = tile([P, 2, R], U8, "wc_sc")
-        nc.vector.tensor_copy(
-            wc_sc[:].bitcast(I32).rearrange("p a (t b) -> p a t b", t=4),
-            wcs_raw[:].bitcast(I32).rearrange("p a (b t) -> p a t b", t=4),
-        )
-
-        tgot = tile([P, 2 * J], U32, "tgot")
-        nc.vector.tensor_copy(tgot[:], twin[:].bitcast(U32).indirect(offsets[:]))
-        tcodes = tile([P, 2, 4 * J], U8, "tcodes")
-        nc.vector.tensor_copy(tcodes[:].bitcast(U16), tgot[:].bitcast(U16).rearrange("p (j d) -> p d j", d=2))
 
         w_codes = [[tile([P, 2 * P], U32, "w_codes%d_%d" % (a, u)) for u in range(2)] for a in range(2)]
         w_sc = [[tile([P, 2 * P], U8, "w_sc%d_%d" % (a, u)) for u in range(2)] for a in range(2)]
@@ -114,11 +103,16 @@ def tile_list_pnet_res_kernel(
         cast_w(0, 0, nc.scalar.copy)
         cast_w(0, 1, nc.scalar.copy)
         quant_w(0, 0)
+        wc_sc = sb.tile([P, 2, R], U8, name="wc_sc", tag="got", align_bytes=64)
+        nc.vector.tensor_copy(
+            wc_sc[:].bitcast(I32).rearrange("p a (t b) -> p a t b", t=4),
+            wcs_raw[:].bitcast(I32).rearrange("p a (b t) -> p a t b", t=4),
+        )
         quant_w(0, 1)
         cast_w(1, 0, nc.scalar.copy)
         cast_w(1, 1, nc.vector.tensor_copy)
-        quant_w(1, 0)
         quant_w(1, 1)
+        quant_w(1, 0)
 
         nb = [ [ps.tile([P, 4, JB], F32, name="nb%d_%d" % (g, b), tag="bank%d" % (4 * g + b)) for b in range(4)] for g in range(2)]
         for b in range(4):
@@ -145,96 +139,107 @@ def tile_list_pnet_res_kernel(
             )
             return g
 
-        c_codes = [[tile([P, J // 2], U32, "c_codes%d_%d" % (a, hf)) for hf in range(2)] for a in range(2)]
-        c_sc = [[tile([P, J // 2], U8, "c_sc%d_%d" % (a, hf)) for hf in range(2)] for a in range(2)]
+        def quantise(g, width, name):
+            codes = tile([P, width], U32, name + "_codes")
+            scales = tile([P, width], U8, name + "_scales")
+            nc.vector.quantize_mx(codes[:].bitcast(FP8X4), scales[:], g[:])
+            return codes, scales
 
-        def quant_c(a, hf, g):
-            nc.vector.quantize_mx(c_codes[a][hf][:].bitcast(FP8X4), c_sc[a][hf][:], g[:])
-
+        spent = [c0_raw[:, 0:2, 0:256], c0_raw[:, 2:4, 0:256], c1_raw[0][:, 0:2, :], c1_raw[0][:, 2:4, :]]
+        firsts = [x.rearrange("p u (j t) -> p u j t", t=4) for x in spent]
         pooled = [tile([P, 4 * JB], F32, "pooled%d" % b) for b in range(4)]
 
+        def copy_first(b):
+            nc.scalar.copy(firsts[b], nb[0][b][:].rearrange("p t (u j) -> p u j t", u=2))
+
         def pool_max(b):
-            first = tile([P, 4 * JB], F32, "first%d" % b)
-            nc.scalar.copy(first[:].rearrange("p (j t) -> p j t", t=4), nb[0][b][:].rearrange("p t j -> p j t"))
             nc.vector.tensor_tensor(
-                pooled[b][:].rearrange("p (j t) -> p j t", t=4),
-                nb[1][b][:].rearrange("p t j -> p j t"),
-                first[:].rearrange("p (j t) -> p j t", t=4),
+                pooled[b][:].rearrange("p (u j t) -> p u j t", u=2, t=4),
+                nb[1][b][:].rearrange("p t (u j) -> p u j t", u=2),
+                firsts[b],
                 ALU.max,
             )
 
-        g00 = interleave(c0_raw[:, :, 0:256], 256, "cg00", nc.scalar.copy)
-        g01 = interleave(c0_raw[:, :, 256:512], 256, "cg01", nc.vector.tensor_copy)
-        quant_c(0, 0, g00)
-        quant_c(0, 1, g01)
-        pool_max(0)
-        quant_c(1, 0, interleave(c1_raw[0], 256, "cg10", nc.scalar.copy))
-        pool_max(1)
-        pool_max(2)
-        pool_max(3)
-        quant_c(1, 1, interleave(c1_raw[1], 256, "cg11", nc.vector.tensor_copy))
-        wdg = interleave(wd_raw, N, "wdg", nc.scalar.copy)
-
-        hb = [tile([P, 8 * JB], BF16, "hb%d" % hf) for hf in range(2)]
-        hr = [tile([P, 8 * JB], BF16, "hr%d" % hf) for hf in range(2)]
-        wd_codes = tile([P, N], U32, "wd_codes")
-        wd_sc = tile([P, N], U8, "wd_sc")
-        ys = [None, None]
-
-        def own_add(b):
-            hf, bb = divmod(b, 2)
+        def own_add(b, operands, h_sum):
             own = ps.tile([P, 4, JB], F32, name="own%d" % b, tag="bank%d" % b)
             for a in range(2):
+                (codes, scales), j0 = operands[a]
                 for t in range(4):
                     nc.tensor.matmul_mx(
                         own[:, t, :],
                         lhsT=wc_codes[:, a, 2 * P * t : 2 * P * (t + 1)].bitcast(FP4X4),
                         lhsT_scale=wc_sc[:, a, P * t : P * (t + 1)],
-                        rhs=c_codes[a][hf][:, JB * bb : JB * (bb + 1)].bitcast(FP8X4),
-                        rhs_scale=c_sc[a][hf][:, JB * bb : JB * (bb + 1)],
+                        rhs=codes[:, j0 : j0 + JB].bitcast(FP8X4),
+                        rhs_scale=scales[:, j0 : j0 + JB],
                         start=(a == 0 and t == 0),
                         stop=(a == 1 and t == 3),
                     )
             nc.vector.tensor_tensor(
-                hb[hf][:, 512 * bb : 512 * (bb + 1)].rearrange("p (j t) -> p j t", t=4),
+                h_sum.rearrange("p (j t) -> p j t", t=4),
                 own[:].rearrange("p t j -> p j t"),
                 pooled[b][:].rearrange("p (j t) -> p j t", t=4),
                 ALU.add,
             )
 
-        def relu(hf):
-            nc.vector.tensor_scalar_max(hr[hf][:], hb[hf][:], 0.0)
-
-        def second(hf):
-            h_codes = tile([P, 2 * JB], U32, "h_codes%d" % hf)
-            h_sc = tile([P, 2 * JB], U8, "h_sc%d" % hf)
-            nc.vector.quantize_mx(h_codes[:].bitcast(FP8X4), h_sc[:], hr[hf][:])
-            y = ps.tile([P, 2, 2 * JB], F32, name="y%d" % hf, tag="bank%d" % (4 + hf))
+        def second(n, h, width):
+            codes, scales = quantise(h, width, "h%d" % n)
+            y = ps.tile([P, 2, width], F32, name="y%d" % n, tag="bank%d" % (4 + n))
             for nh in range(2):
                 nc.tensor.matmul_mx(
                     y[:, nh, :],
                     lhsT=wd_codes[:, P * nh : P * (nh + 1)].bitcast(FP8X4),
                     lhsT_scale=wd_sc[:, P * nh : P * (nh + 1)],
-                    rhs=h_codes[:].bitcast(FP8X4),
-                    rhs_scale=h_sc[:],
+                    rhs=codes[:].bitcast(FP8X4),
+                    rhs_scale=scales[:],
                     start=True,
                     stop=True,
                 )
             return y
 
-        def finish(hf, y):
-            o = tile([P, 2, 2 * JB], F32, "o%d" % hf)
-            nc.vector.tensor_tensor(o[:], y[:], res_sb[:, :, 256 * hf : 256 * (hf + 1)], ALU.add)
-            nc.sync.dma_start(out.rearrange("(h p) j -> p h j", h=2)[:, :, 256 * hf : 256 * (hf + 1)], o[:])
+        def finish(n, y, j0, width):
+            o = tile([P, 2, width], F32, "o%d" % n)
+            nc.vector.tensor_tensor(o[:], y[:], res_sb[:, :, j0 : j0 + width], ALU.add)
+            nc.sync.dma_start(out.rearrange("(h p) j -> p h j", h=2)[:, :, j0 : j0 + width], o[:])
 
-        own_add(0)
-        own_add(1)
-        relu(0)
-        own_add(2)
-        own_add(3)
-        nc.vector.quantize_mx(wd_codes[:].bitcast(FP8X4), wd_sc[:], wdg[:])
-        y0 = second(0)
-        relu(1)
-        finish(0, y0)
-        y1 = second(1)
-        finish(1, y1)
+        g00 = interleave(c0_raw[:, :, 0:256], 256, "cg00", nc.scalar.copy)
+        g01 = interleave(c0_raw[:, :, 256:512], 256, "cg01", nc.vector.tensor_copy)
+        wc_codes = tile([P, 2, 2 * R], U8, "wc_codes")
+        nc.vector.tensor_copy(
+            wc_codes[:].bitcast(I32).rearrange("p a (t b e) -> p a t b e", t=4, e=2),
+            wcw_raw[:].rearrange("p a (b t e) -> p a t b e", t=4, e=2),
+        )
+
+        copy_first(0)
+        q01 = quantise(g01, 256, "c01")
+        q00 = quantise(g00, 256, "c00")
+        copy_first(1)
+        pool_max(0)
+        g10 = interleave(c1_raw[0], 256, "cg10", nc.scalar.copy)
+        pool_max(1)
+        copy_first(2)
+        q10 = quantise(g10, 256, "c10")
+        copy_first(3)
+        pool_max(2)
+        pool_max(3)
+        g12 = interleave(c1_raw[1][:, :, 0:128], 128, "cg12", nc.scalar.copy)
+        g13 = interleave(c1_raw[1][:, :, 128:256], 128, "cg13", nc.scalar.copy)
+        wdg = interleave(wd_raw, N, "wdg", nc.scalar.copy)
+        widths = [256, 128, 128]
+        sums = [tile([P, 4 * x], BF16, "sum%d" % n) for n, x in enumerate(widths)]
+        hs = [tile([P, 4 * x], BF16, "h%d" % n) for n, x in enumerate(widths)]
+        q12 = quantise(g12, 128, "c12")
+        own_add(0, [(q00, 0), (q10, 0)], sums[0][:, 0:512])
+        q13 = quantise(g13, 128, "c13")
+        own_add(1, [(q00, 128), (q10, 128)], sums[0][:, 512:1024])
+        own_add(2, [(q01, 0), (q12, 0)], sums[1][:])
+        nc.scalar.activation(hs[0][:], sums[0][:], mybir.ActivationFunctionType.Relu)
+        wd_codes, wd_sc = quantise(wdg, N, "wd")
+        own_add(3, [(q01, 128), (q13, 0)], sums[2][:])
+        nc.scalar.activation(hs[1][:], sums[1][:], mybir.ActivationFunctionType.Relu)
+        y0 = second(0, hs[0], 256)
+        nc.vector.tensor_scalar_max(hs[2][:], sums[2][:], 0.0)
+        y1 = second(1, hs[1], 128)
+        y2 = second(2, hs[2], 128)
+        finish(0, y0, 0, 256)
+        finish(1, y1, 256, 128)
+        finish(2, y2, 384, 128)

@@ -224,22 +224,18 @@ def tile_list_pnet_res_kernel(
         g12 = interleave(c1_raw[1][:, :, 0:128], 128, "cg12", nc.scalar.copy)
         g13 = interleave(c1_raw[1][:, :, 128:256], 128, "cg13", nc.scalar.copy)
         wdg = interleave(wd_raw, N, "wdg", nc.scalar.copy)
-        widths = [256, 128, 128]
-        sums = [tile([P, 4 * x], BF16, "sum%d" % n) for n, x in enumerate(widths)]
-        hs = [tile([P, 4 * x], BF16, "h%d" % n) for n, x in enumerate(widths)]
+        sums = [tile([P, 4 * JB], BF16, "sum%d" % b) for b in range(4)]
+        hs = [tile([P, 4 * JB], BF16, "h%d" % b) for b in range(4)]
         q12 = quantise(g12, 128, "c12")
-        own_add(0, [(q00, 0), (q10, 0)], sums[0][:, 0:512])
+        own_add(0, [(q00, 0), (q10, 0)], sums[0][:])
         q13 = quantise(g13, 128, "c13")
-        own_add(1, [(q00, 128), (q10, 128)], sums[0][:, 512:1024])
-        own_add(2, [(q01, 0), (q12, 0)], sums[1][:])
-        nc.scalar.activation(hs[0][:], sums[0][:], mybir.ActivationFunctionType.Relu)
+        own_add(1, [(q00, 128), (q10, 128)], sums[1][:])
+        own_add(2, [(q01, 0), (q12, 0)], sums[2][:])
         wd_codes, wd_sc = quantise(wdg, N, "wd")
-        own_add(3, [(q01, 128), (q13, 0)], sums[2][:])
-        nc.scalar.activation(hs[1][:], sums[1][:], mybir.ActivationFunctionType.Relu)
-        y0 = second(0, hs[0], 256)
-        nc.vector.tensor_scalar_max(hs[2][:], sums[2][:], 0.0)
-        y1 = second(1, hs[1], 128)
-        y2 = second(2, hs[2], 128)
-        finish(0, y0, 0, 256)
-        finish(1, y1, 256, 128)
-        finish(2, y2, 384, 128)
+        own_add(3, [(q01, 128), (q13, 0)], sums[3][:])
+        for b in range(3):
+            nc.scalar.activation(hs[b][:], sums[b][:], mybir.ActivationFunctionType.Relu)
+        nc.vector.tensor_scalar_max(hs[3][:], sums[3][:], 0.0)
+        ys = [second(b, hs[b], JB) for b in range(4)]
+        for b in range(4):
+            finish(b, ys[b], JB * b, JB)

@@ -60,6 +60,23 @@ def tile_list_pnet_res_kernel(
         tcodes = tile([P, 2, 4 * J], U8, "tcodes")
         nc.vector.tensor_copy(tcodes[:].bitcast(U16), tgot[:].bitcast(U16).rearrange("p (j d) -> p d j", d=2))
 
+        zeros = tile([P, 4 * P], BF16, "zeros")
+        nc.vector.memset(zeros[:], 0.0)
+        zero_codes = tile([P, P], U32, "zero_codes")
+        zero_scales = tile([P, P], U8, "zero_scales")
+        nc.vector.quantize_mx(zero_codes[:].bitcast(FP8X4), zero_scales[:], zeros[:])
+        warm = ps.tile([P, 512], F32, name="warm", tag="bank7")
+        for width in (512, 512, 256):
+            nc.tensor.matmul_mx(
+                warm[:, 0:width],
+                lhsT=zero_codes[:].bitcast(FP8X4),
+                lhsT_scale=zero_scales[:],
+                rhs=tgot[:].bitcast(U8)[:, 0 : 2 * width].bitcast(FP4X4),
+                rhs_scale=sgot[:, 0:width],
+                start=True,
+                stop=True,
+            )
+
         def move_plane(a, queue):
             for q in range(4):
                 queue.dma_start(

@@ -40,25 +40,29 @@ def tile_list_pnet_res_kernel(
         nc.sync.dma_start(w0_raw[:], w[0:512, :].rearrange("(p i) r -> p (i r)", i=4))
 
         wcs_raw = tile([P, 2, R], U8, "wcs_raw")
-        nc.vector.memset(wcs_raw[:].rearrange("p a r -> p (a r)").bitcast(I32), 0)
+        nc.gpsimd.memset(wcs_raw[:].rearrange("p a r -> p (a r)").bitcast(I32), 0)
         nc.vector.memset(swin[32:64, :].bitcast(I32), 0)
         nc.vector.memset(swin[64:128, :].bitcast(I32), 0)
         tplane = [tile([P, 2 * J], U8, "tplane%d" % a) for a in range(2)]
-        for a in range(2):
-            nc.vector.memset(tplane[a][:].bitcast(I32), 0)
+        nc.vector.memset(tplane[1][:].bitcast(I32), 0)
         for q in range(4):
-            nc.scalar.dma_start(
+            nc.gpsimd.dma_start(
                 wcs_raw[32 * q : 32 * q + 4, :, :].bitcast(I32),
                 wc_scales[:, 4 * q : 4 * q + 4, :].rearrange("a s r -> s a r").bitcast(I32),
             )
 
         sgot = tile([P, 2 * J], U8, "sgot")
         nc.vector.tensor_copy(sgot[:], swin[:].indirect(offsets[:]))
+        nc.vector.tensor_copy(tplane[0][:].bitcast(I32), sgot[:].bitcast(I32))
 
         tgot = sb.tile([P, 2 * J], U32, name="tgot", tag="got", align_bytes=64)
-        nc.vector.tensor_copy(tgot[:], twin[:].bitcast(U32).indirect(offsets[:]))
-        tcodes = tile([P, 2, 4 * J], U8, "tcodes")
-        nc.vector.tensor_copy(tcodes[:].bitcast(U16), tgot[:].bitcast(U16).rearrange("p (j d) -> p d j", d=2))
+        tcodes = [tile([P, 2, 2 * J], U8, "tcodes%d" % g) for g in range(2)]
+        for g in range(2):
+            nc.vector.tensor_copy(tgot[:, J * g : J * (g + 1)], twin[:].bitcast(U32).indirect(offsets[:, 32 * g : 32 * (g + 1)]))
+        for g in range(2):
+            nc.vector.tensor_copy(
+                tcodes[g][:].bitcast(U16), tgot[:, J * g : J * (g + 1)].bitcast(U16).rearrange("p (j d) -> p d j", d=2)
+            )
 
         zeros = tile([P, 4 * P], BF16, "zeros")
         nc.vector.memset(zeros[:], 0.0)
@@ -71,31 +75,33 @@ def tile_list_pnet_res_kernel(
                 warm[:, 0:width],
                 lhsT=zero_codes[:].bitcast(FP8X4),
                 lhsT_scale=zero_scales[:],
-                rhs=tgot[:].bitcast(U8)[:, 0 : 2 * width].bitcast(FP4X4),
+                rhs=tgot[:, J:].bitcast(U8)[:, 0 : 2 * width].bitcast(FP4X4),
                 rhs_scale=sgot[:, 0:width],
                 start=True,
                 stop=True,
             )
 
-        def move_plane(a, queue):
-            for q in range(4):
-                queue.dma_start(
-                    tplane[a][32 * q : 32 * q + 4, :].bitcast(I32),
-                    sgot[16 * a + 4 * q : 16 * a + 4 * q + 4, :].bitcast(I32),
-                )
+        def move_rows(a, q, queue):
+            queue.dma_start(
+                tplane[a][32 * q : 32 * q + 4, :].bitcast(I32),
+                sgot[16 * a + 4 * q : 16 * a + 4 * q + 4, :].bitcast(I32),
+            )
 
-        late = sb.tile([P, 8192], F32, name="late", tag="shared", align_bytes=64)
-        move_plane(0, nc.sync)
-        w1_raw = late[:, 0:2048]
+        w1_tile = tile([P, 4 * R], F32, "w1_raw")
+        w1_raw = w1_tile[:]
         nc.sync.dma_start(w1_raw, w[512:1024, :].rearrange("(p i) r -> p (i r)", i=4))
-        move_plane(1, nc.sync)
+        move_rows(1, 0, nc.sync)
+        for a in range(2):
+            for q in range(1, 4):
+                move_rows(a, q, nc.scalar)
         w_raw = [w0_raw[:], w1_raw]
+        late = tile([P, 8192], F32, "late")
         nc.sync.dma_start(late[:, 2048:4096], c[0:512, :].rearrange("(p i) j -> p (i j)", i=4))
         c0_raw = late[:, 2048:4096].rearrange("p (i j) -> p i j", i=4)
         c1_raw = [late[:, 4096 + 1024 * hf : 4096 + 1024 * (hf + 1)].rearrange("p (i j) -> p i j", i=4) for hf in range(2)]
-        nc.sync.dma_start(c1_raw[0], c[512:1024, 0:256].rearrange("(p i) j -> p i j", i=4))
-        wcw_raw = sb.tile([P, 2, R // 2], I32, name="wcw_raw", tag="words", align_bytes=64)
+        wcw_raw = tile([P, 2, R // 2], I32, "wcw_raw")
         nc.sync.dma_start(wcw_raw[:], wc_words.rearrange("a p b -> p a b").bitcast(I32))
+        nc.sync.dma_start(c1_raw[0], c[512:1024, 0:256].rearrange("(p i) j -> p i j", i=4))
         nc.sync.dma_start(c1_raw[1], c[512:1024, 256:512].rearrange("(p i) j -> p i j", i=4))
         wd_raw = late[:, 6144:7168].rearrange("p (i j) -> p i j", i=4)
         wd_v = wd.rearrange("(b t e) n -> t b e n", t=4, e=4)
@@ -106,7 +112,7 @@ def tile_list_pnet_res_kernel(
 
         w_codes = [[tile([P, 2 * P], U32, "w_codes%d_%d" % (a, u)) for u in range(2)] for a in range(2)]
         w_sc = [[tile([P, 2 * P], U8, "w_sc%d_%d" % (a, u)) for u in range(2)] for a in range(2)]
-        wg = [[tile([P, 8 * P], BF16, "wg%d_%d" % (a, u)) for u in range(2)] for a in range(2)]
+        wg = [[sb.tile([P, 8 * P], BF16, name="wg%d_%d" % (a, u), tag="wg%d_%d" % (a, a * u), align_bytes=64) for u in range(2)] for a in range(2)]
 
         def cast_w(a, u, copy):
             copy(
@@ -118,38 +124,40 @@ def tile_list_pnet_res_kernel(
             nc.vector.quantize_mx(w_codes[a][u][:].bitcast(FP8X4), w_sc[a][u][:], wg[a][u][:])
 
         cast_w(0, 0, nc.scalar.copy)
-        cast_w(0, 1, nc.scalar.copy)
         quant_w(0, 0)
-        wc_sc = sb.tile([P, 2, R], U8, name="wc_sc", tag="got", align_bytes=64)
-        nc.vector.tensor_copy(
-            wc_sc[:].bitcast(I32).rearrange("p a (t b) -> p a t b", t=4),
-            wcs_raw[:].bitcast(I32).rearrange("p a (b t) -> p a t b", t=4),
-        )
+        cast_w(0, 1, nc.vector.tensor_copy)
         quant_w(0, 1)
         cast_w(1, 0, nc.scalar.copy)
         cast_w(1, 1, nc.vector.tensor_copy)
         quant_w(1, 1)
         quant_w(1, 0)
+        wc_sc = sb.tile([P, 2, R], U8, name="wc_sc", tag="wg1_0", align_bytes=64)
+        nc.vector.tensor_copy(
+            wc_sc[:].bitcast(I32).rearrange("p a (t b) -> p a t b", t=4),
+            wcs_raw[:].bitcast(I32).rearrange("p a (b t) -> p a t b", t=4),
+        )
 
         nb = [ [ps.tile([P, 4, JB], F32, name="nb%d_%d" % (g, b), tag="bank%d" % (4 * g + b)) for b in range(4)] for g in range(2)]
-        for b in range(4):
-            for a in range(2):
+        for a, b in [(0, 0), (0, 1), (0, 2), (1, 0), (1, 1), (1, 2), (1, 3), (0, 3)]:
+            if True:
                 for g in range(2):
                     cols = slice(J * g + JB * b, J * g + JB * (b + 1))
-                    for t in range(4):
+                    order = (2, 3, 0, 1) if a else (0, 1, 2, 3)
+                    opens = a == (1 if b == 3 else 0)
+                    for t in order:
                         wcols = slice(P * (t % 2), P * (t % 2 + 1))
                         nc.tensor.matmul_mx(
                             nb[g][b][:, t, :],
                             lhsT=w_codes[a][t // 2][:, wcols].bitcast(FP8X4),
                             lhsT_scale=w_sc[a][t // 2][:, wcols],
-                            rhs=tcodes[:, a, 2 * cols.start : 2 * cols.stop].bitcast(FP4X4),
+                            rhs=tcodes[g][:, a, 2 * JB * b : 2 * JB * (b + 1)].bitcast(FP4X4),
                             rhs_scale=tplane[a][:, cols],
-                            start=(a == 0 and t == 0),
-                            stop=(a == 1 and t == 3),
+                            start=(opens and t == order[0]),
+                            stop=(not opens and t == order[3]),
                         )
 
         def interleave(raw, width, name, copy):
-            g = tile([P, 4 * width], BF16, name)
+            g = sb.tile([P, 4 * width], BF16, name=name, tag=name, align_bytes=64)
             copy(
                 g[:].rearrange("p (u v i) -> p u i v", v=4, i=4),
                 raw.rearrange("p i (u v) -> p u i v", v=4),
@@ -162,11 +170,14 @@ def tile_list_pnet_res_kernel(
             nc.vector.quantize_mx(codes[:].bitcast(FP8X4), scales[:], g[:])
             return codes, scales
 
-        spent = [c0_raw[:, 0:2, 0:256], c0_raw[:, 2:4, 0:256], c1_raw[0][:, 0:2, :], c1_raw[0][:, 2:4, :]]
+        spent = [c0_raw[:, 0:2, 0:256], c0_raw[:, 2:4, 0:256]]
         firsts = [x.rearrange("p u (j t) -> p u j t", t=4) for x in spent]
         pooled = [tile([P, 4 * JB], F32, "pooled%d" % b) for b in range(4)]
 
         def copy_first(b):
+            if b >= 2:
+                fresh = sb.tile([P, 2, 256], F32, name="first%d" % b, tag="cg00" if b == 2 else "first3", align_bytes=64)
+                firsts.append(fresh[:].rearrange("p u (j t) -> p u j t", t=4))
             nc.scalar.copy(firsts[b], nb[0][b][:].rearrange("p t (u j) -> p u j t", u=2))
 
         def pool_max(b):
@@ -231,12 +242,12 @@ def tile_list_pnet_res_kernel(
         q00 = quantise(g00, 256, "c00")
         copy_first(1)
         pool_max(0)
-        g10 = interleave(c1_raw[0], 256, "cg10", nc.scalar.copy)
-        pool_max(1)
         copy_first(2)
+        g10 = interleave(c1_raw[0], 256, "cg10", nc.vector.tensor_copy)
+        pool_max(1)
         q10 = quantise(g10, 256, "c10")
-        copy_first(3)
         pool_max(2)
+        copy_first(3)
         pool_max(3)
         g12 = interleave(c1_raw[1][:, :, 0:128], 128, "cg12", nc.scalar.copy)
         g13 = interleave(c1_raw[1][:, :, 128:256], 128, "cg13", nc.scalar.copy)

@@ -39,21 +39,21 @@ def tile_list_pnet_res_kernel(
         w0_raw = tile([P, 4 * R], F32, "w0_raw")
         nc.sync.dma_start(w0_raw[:], w[0:512, :].rearrange("(p i) r -> p (i r)", i=4))
 
-        wcs_raw = tile([P, 2, R], U8, "wcs_raw")
-        nc.gpsimd.memset(wcs_raw[:].rearrange("p a r -> p (a r)").bitcast(I32), 0)
+        wcs_raw = tile([32, R], U8, "wcs_raw")
+        nc.scalar.dma_start(wcs_raw[:].bitcast(I32), wc_scales.rearrange("a q r -> (a q) r").bitcast(I32))
         nc.vector.memset(swin[32:64, :].bitcast(I32), 0)
         nc.vector.memset(swin[64:128, :].bitcast(I32), 0)
-        tplane = [tile([P, 2 * J], U8, "tplane%d" % a) for a in range(2)]
+        tplane = [tile([P, 2 * J + R], U8, "tplane%d" % a) for a in range(2)]
+        nc.vector.memset(tplane[0][:, 2 * J :].bitcast(I32), 0)
         nc.vector.memset(tplane[1][:].bitcast(I32), 0)
-        for q in range(4):
-            nc.gpsimd.dma_start(
-                wcs_raw[32 * q : 32 * q + 4, :, :].bitcast(I32),
-                wc_scales[:, 4 * q : 4 * q + 4, :].rearrange("a s r -> s a r").bitcast(I32),
-            )
+        nc.vector.tensor_copy(
+            tplane[0][0:32, 2 * J :].bitcast(I32).rearrange("p (t b) -> p t b", t=4),
+            wcs_raw[:].bitcast(I32).rearrange("p (b t) -> p t b", t=4),
+        )
 
         sgot = tile([P, 2 * J], U8, "sgot")
         nc.vector.tensor_copy(sgot[:], swin[:].indirect(offsets[:]))
-        nc.vector.tensor_copy(tplane[0][:].bitcast(I32), sgot[:].bitcast(I32))
+        nc.vector.tensor_copy(tplane[0][:, 0 : 2 * J].bitcast(I32), sgot[:].bitcast(I32))
 
         tgot = sb.tile([P, 2 * J], U32, name="tgot", tag="got", align_bytes=64)
         tcodes = [tile([P, 2, 2 * J], U8, "tcodes%d" % g) for g in range(2)]
@@ -64,7 +64,7 @@ def tile_list_pnet_res_kernel(
                 tcodes[g][:].bitcast(U16), tgot[:, J * g : J * (g + 1)].bitcast(U16).rearrange("p (j d) -> p d j", d=2)
             )
 
-        zeros = tile([P, 4 * P], BF16, "zeros")
+        zeros = sb.tile([P, 4 * P], BF16, name="zeros", tag="shared", align_bytes=64)
         nc.vector.memset(zeros[:], 0.0)
         zero_codes = tile([P, P], U32, "zero_codes")
         zero_scales = tile([P, P], U8, "zero_scales")
@@ -84,7 +84,7 @@ def tile_list_pnet_res_kernel(
         def move_rows(a, q, queue):
             queue.dma_start(
                 tplane[a][32 * q : 32 * q + 4, :].bitcast(I32),
-                sgot[16 * a + 4 * q : 16 * a + 4 * q + 4, :].bitcast(I32),
+                tplane[0][16 * a + 4 * q : 16 * a + 4 * q + 4, :].bitcast(I32),
             )
 
         w1_tile = tile([P, 4 * R], F32, "w1_raw")
@@ -131,11 +131,6 @@ def tile_list_pnet_res_kernel(
         cast_w(1, 1, nc.vector.tensor_copy)
         quant_w(1, 1)
         quant_w(1, 0)
-        wc_sc = sb.tile([P, 2, R], U8, name="wc_sc", tag="wg1_0", align_bytes=64)
-        nc.vector.tensor_copy(
-            wc_sc[:].bitcast(I32).rearrange("p a (t b) -> p a t b", t=4),
-            wcs_raw[:].bitcast(I32).rearrange("p a (b t) -> p a t b", t=4),
-        )
 
         nb = [ [ps.tile([P, 4, JB], F32, name="nb%d_%d" % (g, b), tag="bank%d" % (4 * g + b)) for b in range(4)] for g in range(2)]
         for a, b in [(0, 0), (0, 1), (0, 2), (1, 0), (1, 1), (1, 2), (1, 3), (0, 3)]:
@@ -196,7 +191,7 @@ def tile_list_pnet_res_kernel(
                     nc.tensor.matmul_mx(
                         own[:, t, :],
                         lhsT=wc_codes[:, a, 2 * P * t : 2 * P * (t + 1)].bitcast(FP4X4),
-                        lhsT_scale=wc_sc[:, a, P * t : P * (t + 1)],
+                        lhsT_scale=tplane[a][:, 2 * J + P * t : 2 * J + P * (t + 1)],
                         rhs=codes[:, j0 : j0 + JB].bitcast(FP8X4),
                         rhs_scale=scales[:, j0 : j0 + JB],
                         start=(a == 0 and t == 0),

@@ -44,16 +44,17 @@ def tile_list_pnet_res_kernel(
         nc.vector.memset(swin[32:64, :].bitcast(I32), 0)
         nc.vector.memset(swin[64:128, :].bitcast(I32), 0)
         tplane = [tile([P, 2 * J + R], U8, "tplane%d" % a) for a in range(2)]
-        nc.vector.memset(tplane[0][:, 2 * J :].bitcast(I32), 0)
-        nc.vector.memset(tplane[1][:].bitcast(I32), 0)
+        for a in range(2):
+            nc.vector.memset(tplane[a][:].bitcast(I32), 0)
+        rows = tile([32, 2 * J + R], U8, "rows")
         nc.vector.tensor_copy(
-            tplane[0][0:32, 2 * J :].bitcast(I32).rearrange("p (t b) -> p t b", t=4),
+            rows[:, 2 * J :].bitcast(I32).rearrange("p (t b) -> p t b", t=4),
             wcs_raw[:].bitcast(I32).rearrange("p (b t) -> p t b", t=4),
         )
 
         sgot = tile([P, 2 * J], U8, "sgot")
         nc.vector.tensor_copy(sgot[:], swin[:].indirect(offsets[:]))
-        nc.vector.tensor_copy(tplane[0][:, 0 : 2 * J].bitcast(I32), sgot[:].bitcast(I32))
+        nc.vector.tensor_copy(rows[:, 0 : 2 * J].bitcast(I32), sgot[0:32, :].bitcast(I32))
 
         tgot = sb.tile([P, 2 * J], U32, name="tgot", tag="got", align_bytes=64)
         tcodes = [tile([P, 2, 2 * J], U8, "tcodes%d" % g) for g in range(2)]
@@ -83,17 +84,17 @@ def tile_list_pnet_res_kernel(
 
         def move_rows(a, q, queue):
             queue.dma_start(
-                tplane[a][32 * q : 32 * q + 4, :].bitcast(I32),
-                tplane[0][16 * a + 4 * q : 16 * a + 4 * q + 4, :].bitcast(I32),
+                tplane[a][q:P:32, :].bitcast(I32),
+                rows[16 * a + q : 16 * (a + 1) : 4, :].bitcast(I32),
             )
 
+        for q in range(4):
+            move_rows(0, q, nc.sync)
         w1_tile = tile([P, 4 * R], F32, "w1_raw")
         w1_raw = w1_tile[:]
         nc.sync.dma_start(w1_raw, w[512:1024, :].rearrange("(p i) r -> p (i r)", i=4))
-        move_rows(1, 0, nc.sync)
-        for a in range(2):
-            for q in range(1, 4):
-                move_rows(a, q, nc.scalar)
+        for q in range(4):
+            move_rows(1, q, nc.sync)
         w_raw = [w0_raw[:], w1_raw]
         late = tile([P, 8192], F32, "late")
         nc.sync.dma_start(late[:, 2048:4096], c[0:512, :].rearrange("(p i) j -> p (i j)", i=4))
@@ -170,9 +171,10 @@ def tile_list_pnet_res_kernel(
         pooled = [tile([P, 4 * JB], F32, "pooled%d" % b) for b in range(4)]
 
         def copy_first(b):
-            if b >= 2:
-                fresh = sb.tile([P, 2, 256], F32, name="first%d" % b, tag="cg00" if b == 2 else "first3", align_bytes=64)
+            if b == 2:
+                fresh = sb.tile([P, 2, 256], F32, name="first2", tag="cg00", align_bytes=64)
                 firsts.append(fresh[:].rearrange("p u (j t) -> p u j t", t=4))
+                firsts.append(c1_raw[0][:, 0:2, :].rearrange("p u (j t) -> p u j t", t=4))
             nc.scalar.copy(firsts[b], nb[0][b][:].rearrange("p t (u j) -> p u j t", u=2))
 
         def pool_max(b):
@@ -185,7 +187,8 @@ def tile_list_pnet_res_kernel(
 
         def own_add(b, operands, h_sum):
             own = ps.tile([P, 4, JB], F32, name="own%d" % b, tag="bank%d" % b)
-            for a in range(2):
+            passes = (0, 1) if b < 2 else (1, 0)
+            for a in passes:
                 (codes, scales), j0 = operands[a]
                 for t in range(4):
                     nc.tensor.matmul_mx(
@@ -194,8 +197,8 @@ def tile_list_pnet_res_kernel(
                         lhsT_scale=tplane[a][:, 2 * J + P * t : 2 * J + P * (t + 1)],
                         rhs=codes[:, j0 : j0 + JB].bitcast(FP8X4),
                         rhs_scale=scales[:, j0 : j0 + JB],
-                        start=(a == 0 and t == 0),
-                        stop=(a == 1 and t == 3),
+                        start=(a == passes[0] and t == 0),
+                        stop=(a == passes[1] and t == 3),
                     )
             nc.vector.tensor_tensor(
                 h_sum.rearrange("p (j t) -> p j t", t=4),

@@ -34,13 +34,13 @@ def tile_list_pnet_res_kernel(
         nc.sync.dma_start(offsets[:], offs)
         swin = sb.tile([P, T], U8, name="swin", tag="shared", align_bytes=64)
         nc.sync.dma_start(swin[0:32, :].bitcast(I32), tab_scales.rearrange("a q t -> (a q) t").bitcast(I32))
+
+        wcs_raw = tile([32, R], U8, "wcs_raw")
+        nc.sync.dma_start(wcs_raw[:].bitcast(I32), wc_scales.rearrange("a q r -> (a q) r").bitcast(I32))
         twin = sb.tile([P, T], I32, name="twin", tag="words", align_bytes=64)
         nc.sync.dma_start(twin[:], tab_words[0].rearrange("p t b -> p (t b)").bitcast(I32))
         w0_raw = tile([P, 4 * R], F32, "w0_raw")
         nc.sync.dma_start(w0_raw[:], w[0:512, :].rearrange("(p i) r -> p (i r)", i=4))
-
-        wcs_raw = tile([32, R], U8, "wcs_raw")
-        nc.scalar.dma_start(wcs_raw[:].bitcast(I32), wc_scales.rearrange("a q r -> (a q) r").bitcast(I32))
         nc.vector.memset(swin[32:64, :].bitcast(I32), 0)
         nc.vector.memset(swin[64:128, :].bitcast(I32), 0)
         tplane = [tile([P, 2 * J + R], U8, "tplane%d" % a) for a in range(2)]
@@ -113,7 +113,7 @@ def tile_list_pnet_res_kernel(
 
         w_codes = [[tile([P, 2 * P], U32, "w_codes%d_%d" % (a, u)) for u in range(2)] for a in range(2)]
         w_sc = [[tile([P, 2 * P], U8, "w_sc%d_%d" % (a, u)) for u in range(2)] for a in range(2)]
-        wg = [[sb.tile([P, 8 * P], BF16, name="wg%d_%d" % (a, u), tag="wg%d_%d" % (a, a * u), align_bytes=64) for u in range(2)] for a in range(2)]
+        wg = [[sb.tile([P, 8 * P], BF16, name="wg%d_%d" % (a, u), tag="wg%d_%d" % (a, u), align_bytes=64) for u in range(2)] for a in range(2)]
 
         def cast_w(a, u, copy):
             copy(
@@ -126,7 +126,7 @@ def tile_list_pnet_res_kernel(
 
         cast_w(0, 0, nc.scalar.copy)
         quant_w(0, 0)
-        cast_w(0, 1, nc.vector.tensor_copy)
+        cast_w(0, 1, nc.scalar.copy)
         quant_w(0, 1)
         cast_w(1, 0, nc.scalar.copy)
         cast_w(1, 1, nc.vector.tensor_copy)
@@ -187,7 +187,7 @@ def tile_list_pnet_res_kernel(
 
         def own_add(b, operands, h_sum):
             own = ps.tile([P, 4, JB], F32, name="own%d" % b, tag="bank%d" % b)
-            passes = (0, 1) if b < 2 else (1, 0)
+            passes = (0, 1) if b < 3 else (1, 0)
             for a in passes:
                 (codes, scales), j0 = operands[a]
                 for t in range(4):

@@ -174,13 +174,13 @@ def tile_list_pnet_res_kernel(
             if b == 2:
                 fresh = sb.tile([P, 2, 256], F32, name="first2", tag="cg00", align_bytes=64)
                 firsts.append(fresh[:].rearrange("p u (j t) -> p u j t", t=4))
-                firsts.append(c1_raw[0][:, 0:2, :].rearrange("p u (j t) -> p u j t", t=4))
-            nc.scalar.copy(firsts[b], nb[0][b][:].rearrange("p t (u j) -> p u j t", u=2))
+                firsts.append(c1_raw[1][:, :, 0:128].rearrange("p u (j t) -> p u j t", t=4))
+            nc.scalar.copy(firsts[b], nb[0][b][:].rearrange("p t (u j) -> p u j t", u=firsts[b].shape[1]))
 
         def pool_max(b):
             nc.vector.tensor_tensor(
-                pooled[b][:].rearrange("p (u j t) -> p u j t", u=2, t=4),
-                nb[1][b][:].rearrange("p t (u j) -> p u j t", u=2),
+                pooled[b][:].rearrange("p (u j t) -> p u j t", u=firsts[b].shape[1], t=4),
+                nb[1][b][:].rearrange("p t (u j) -> p u j t", u=firsts[b].shape[1]),
                 firsts[b],
                 ALU.max,
             )
@@ -240,22 +240,22 @@ def tile_list_pnet_res_kernel(
         q00 = quantise(g00, 256, "c00")
         copy_first(1)
         pool_max(0)
+        g10 = interleave(c1_raw[0], 256, "cg10", nc.scalar.copy)
         copy_first(2)
-        g10 = interleave(c1_raw[0], 256, "cg10", nc.vector.tensor_copy)
         pool_max(1)
         q10 = quantise(g10, 256, "c10")
         pool_max(2)
-        copy_first(3)
-        pool_max(3)
         g12 = interleave(c1_raw[1][:, :, 0:128], 128, "cg12", nc.scalar.copy)
         g13 = interleave(c1_raw[1][:, :, 128:256], 128, "cg13", nc.scalar.copy)
+        copy_first(3)
         wdg = interleave(wd_raw, N, "wdg", nc.scalar.copy)
         sums = [tile([P, 4 * JB], BF16, "sum%d" % b) for b in range(4)]
         hs = [tile([P, 4 * JB], BF16, "h%d" % b) for b in range(4)]
-        q12 = quantise(g12, 128, "c12")
         own_add(0, [(q00, 0), (q10, 0)], sums[0][:])
-        q13 = quantise(g13, 128, "c13")
+        q12 = quantise(g12, 128, "c12")
         own_add(1, [(q00, 128), (q10, 128)], sums[1][:])
+        q13 = quantise(g13, 128, "c13")
+        pool_max(3)
         own_add(2, [(q01, 0), (q12, 0)], sums[2][:])
         wd_codes, wd_sc = quantise(wdg, N, "wd")
         own_add(3, [(q01, 128), (q13, 0)], sums[3][:])

@@ -34,75 +34,51 @@ def tile_list_pnet_res_kernel(
         nc.sync.dma_start(offsets[:], offs)
         swin = sb.tile([P, T], U8, name="swin", tag="shared", align_bytes=64)
         nc.sync.dma_start(swin[0:32, :].bitcast(I32), tab_scales.rearrange("a q t -> (a q) t").bitcast(I32))
-
-        wcs_raw = tile([32, R], U8, "wcs_raw")
-        nc.sync.dma_start(wcs_raw[:].bitcast(I32), wc_scales.rearrange("a q r -> (a q) r").bitcast(I32))
         twin = sb.tile([P, T], I32, name="twin", tag="words", align_bytes=64)
         nc.sync.dma_start(twin[:], tab_words[0].rearrange("p t b -> p (t b)").bitcast(I32))
         w0_raw = tile([P, 4 * R], F32, "w0_raw")
         nc.sync.dma_start(w0_raw[:], w[0:512, :].rearrange("(p i) r -> p (i r)", i=4))
+
+        wcs_raw = tile([P, 2, R], U8, "wcs_raw")
+        nc.gpsimd.memset(wcs_raw[:].rearrange("p a r -> p (a r)").bitcast(I32), 0)
         nc.vector.memset(swin[32:64, :].bitcast(I32), 0)
         nc.vector.memset(swin[64:128, :].bitcast(I32), 0)
-        tplane = [tile([P, 2 * J + R], U8, "tplane%d" % a) for a in range(2)]
+        tplane = [tile([P, 2 * J], U8, "tplane%d" % a) for a in range(2)]
         for a in range(2):
             nc.vector.memset(tplane[a][:].bitcast(I32), 0)
-        rows = tile([32, 2 * J + R], U8, "rows")
-        nc.vector.tensor_copy(
-            rows[:, 2 * J :].bitcast(I32).rearrange("p (t b) -> p t b", t=4),
-            wcs_raw[:].bitcast(I32).rearrange("p (b t) -> p t b", t=4),
-        )
+        for q in range(4):
+            nc.gpsimd.dma_start(
+                wcs_raw[32 * q : 32 * q + 4, :, :].bitcast(I32),
+                wc_scales[:, 4 * q : 4 * q + 4, :].rearrange("a s r -> s a r").bitcast(I32),
+            )
 
         sgot = tile([P, 2 * J], U8, "sgot")
         nc.vector.tensor_copy(sgot[:], swin[:].indirect(offsets[:]))
-        nc.vector.tensor_copy(rows[:, 0 : 2 * J].bitcast(I32), sgot[0:32, :].bitcast(I32))
 
         tgot = sb.tile([P, 2 * J], U32, name="tgot", tag="got", align_bytes=64)
-        tcodes = [tile([P, 2, 2 * J], U8, "tcodes%d" % g) for g in range(2)]
-        for g in range(2):
-            nc.vector.tensor_copy(tgot[:, J * g : J * (g + 1)], twin[:].bitcast(U32).indirect(offsets[:, 32 * g : 32 * (g + 1)]))
-        for g in range(2):
-            nc.vector.tensor_copy(
-                tcodes[g][:].bitcast(U16), tgot[:, J * g : J * (g + 1)].bitcast(U16).rearrange("p (j d) -> p d j", d=2)
-            )
+        nc.vector.tensor_copy(tgot[:], twin[:].bitcast(U32).indirect(offsets[:]))
+        tcodes = tile([P, 2, 4 * J], U8, "tcodes")
+        nc.vector.tensor_copy(tcodes[:].bitcast(U16), tgot[:].bitcast(U16).rearrange("p (j d) -> p d j", d=2))
 
-        zeros = sb.tile([P, 4 * P], BF16, name="zeros", tag="shared", align_bytes=64)
-        nc.vector.memset(zeros[:], 0.0)
-        zero_codes = tile([P, P], U32, "zero_codes")
-        zero_scales = tile([P, P], U8, "zero_scales")
-        nc.vector.quantize_mx(zero_codes[:].bitcast(FP8X4), zero_scales[:], zeros[:])
-        warm = ps.tile([P, 512], F32, name="warm", tag="bank7")
-        for width in (512, 512, 256):
-            nc.tensor.matmul_mx(
-                warm[:, 0:width],
-                lhsT=zero_codes[:].bitcast(FP8X4),
-                lhsT_scale=zero_scales[:],
-                rhs=tgot[:, J:].bitcast(U8)[:, 0 : 2 * width].bitcast(FP4X4),
-                rhs_scale=sgot[:, 0:width],
-                start=True,
-                stop=True,
-            )
+        def move_plane(a, queue):
+            for q in range(4):
+                queue.dma_start(
+                    tplane[a][32 * q : 32 * q + 4, :].bitcast(I32),
+                    sgot[16 * a + 4 * q : 16 * a + 4 * q + 4, :].bitcast(I32),
+                )
 
-        def move_rows(a, q, queue):
-            queue.dma_start(
-                tplane[a][q:P:32, :].bitcast(I32),
-                rows[16 * a + q : 16 * (a + 1) : 4, :].bitcast(I32),
-            )
-
-        for q in range(4):
-            move_rows(0, q, nc.sync)
-        w1_tile = tile([P, 4 * R], F32, "w1_raw")
-        w1_raw = w1_tile[:]
+        late = sb.tile([P, 8192], F32, name="late", tag="shared", align_bytes=64)
+        move_plane(0, nc.sync)
+        w1_raw = late[:, 0:2048]
         nc.sync.dma_start(w1_raw, w[512:1024, :].rearrange("(p i) r -> p (i r)", i=4))
-        for q in range(4):
-            move_rows(1, q, nc.sync)
+        move_plane(1, nc.sync)
         w_raw = [w0_raw[:], w1_raw]
-        late = tile([P, 8192], F32, "late")
         nc.sync.dma_start(late[:, 2048:4096], c[0:512, :].rearrange("(p i) j -> p (i j)", i=4))
         c0_raw = late[:, 2048:4096].rearrange("p (i j) -> p i j", i=4)
         c1_raw = [late[:, 4096 + 1024 * hf : 4096 + 1024 * (hf + 1)].rearrange("p (i j) -> p i j", i=4) for hf in range(2)]
-        wcw_raw = tile([P, 2, R // 2], I32, "wcw_raw")
-        nc.sync.dma_start(wcw_raw[:], wc_words.rearrange("a p b -> p a b").bitcast(I32))
         nc.sync.dma_start(c1_raw[0], c[512:1024, 0:256].rearrange("(p i) j -> p i j", i=4))
+        wcw_raw = sb.tile([P, 2, R // 2], I32, name="wcw_raw", tag="words", align_bytes=64)
+        nc.sync.dma_start(wcw_raw[:], wc_words.rearrange("a p b -> p a b").bitcast(I32))
         nc.sync.dma_start(c1_raw[1], c[512:1024, 256:512].rearrange("(p i) j -> p i j", i=4))
         wd_raw = late[:, 6144:7168].rearrange("p (i j) -> p i j", i=4)
         wd_v = wd.rearrange("(b t e) n -> t b e n", t=4, e=4)
@@ -132,6 +108,11 @@ def tile_list_pnet_res_kernel(
         cast_w(1, 1, nc.vector.tensor_copy)
         quant_w(1, 1)
         quant_w(1, 0)
+        wc_sc = sb.tile([P, 2, R], U8, name="wc_sc", tag="wg1_0", align_bytes=64)
+        nc.vector.tensor_copy(
+            wc_sc[:].bitcast(I32).rearrange("p a (t b) -> p a t b", t=4),
+            wcs_raw[:].bitcast(I32).rearrange("p a (b t) -> p a t b", t=4),
+        )
 
         nb = [ [ps.tile([P, 4, JB], F32, name="nb%d_%d" % (g, b), tag="bank%d" % (4 * g + b)) for b in range(4)] for g in range(2)]
         for a, b in [(0, 0), (0, 1), (0, 2), (1, 0), (1, 1), (1, 2), (1, 3), (0, 3)]:
@@ -146,18 +127,18 @@ def tile_list_pnet_res_kernel(
                             nb[g][b][:, t, :],
                             lhsT=w_codes[a][t // 2][:, wcols].bitcast(FP8X4),
                             lhsT_scale=w_sc[a][t // 2][:, wcols],
-                            rhs=tcodes[g][:, a, 2 * JB * b : 2 * JB * (b + 1)].bitcast(FP4X4),
+                            rhs=tcodes[:, a, 2 * cols.start : 2 * cols.stop].bitcast(FP4X4),
                             rhs_scale=tplane[a][:, cols],
                             start=(opens and t == order[0]),
-                            stop=(not opens and t == order[3]),
+                            stop=(b < 3 and not opens and t == order[3]),
                         )
+
+        def round_into(g, raw, copy):
+            copy(g.rearrange("p (u v i) -> p u i v", v=4, i=4), raw.rearrange("p i (u v) -> p u i v", v=4))
 
         def interleave(raw, width, name, copy):
             g = sb.tile([P, 4 * width], BF16, name=name, tag=name, align_bytes=64)
-            copy(
-                g[:].rearrange("p (u v i) -> p u i v", v=4, i=4),
-                raw.rearrange("p i (u v) -> p u i v", v=4),
-            )
+            round_into(g[:], raw, copy)
             return g
 
         def quantise(g, width, name):
@@ -168,13 +149,12 @@ def tile_list_pnet_res_kernel(
 
         spent = [c0_raw[:, 0:2, 0:256], c0_raw[:, 2:4, 0:256]]
         firsts = [x.rearrange("p u (j t) -> p u j t", t=4) for x in spent]
-        pooled = [tile([P, 4 * JB], F32, "pooled%d" % b) for b in range(4)]
+        pooled = [tile([P, 4 * JB], F32, "pooled%d" % b) for b in range(3)]
 
         def copy_first(b):
             if b == 2:
                 fresh = sb.tile([P, 2, 256], F32, name="first2", tag="cg00", align_bytes=64)
                 firsts.append(fresh[:].rearrange("p u (j t) -> p u j t", t=4))
-                firsts.append(c1_raw[1][:, :, 0:128].rearrange("p u (j t) -> p u j t", t=4))
             nc.scalar.copy(firsts[b], nb[0][b][:].rearrange("p t (u j) -> p u j t", u=firsts[b].shape[1]))
 
         def pool_max(b):
@@ -185,21 +165,37 @@ def tile_list_pnet_res_kernel(
                 ALU.max,
             )
 
-        def own_add(b, operands, h_sum):
-            own = ps.tile([P, 4, JB], F32, name="own%d" % b, tag="bank%d" % b)
-            passes = (0, 1) if b < 3 else (1, 0)
-            for a in passes:
+        def own_passes(own, operands, opens):
+            for a in range(2):
                 (codes, scales), j0 = operands[a]
                 for t in range(4):
                     nc.tensor.matmul_mx(
                         own[:, t, :],
                         lhsT=wc_codes[:, a, 2 * P * t : 2 * P * (t + 1)].bitcast(FP4X4),
-                        lhsT_scale=tplane[a][:, 2 * J + P * t : 2 * J + P * (t + 1)],
+                        lhsT_scale=wc_sc[:, a, P * t : P * (t + 1)],
                         rhs=codes[:, j0 : j0 + JB].bitcast(FP8X4),
                         rhs_scale=scales[:, j0 : j0 + JB],
-                        start=(a == passes[0] and t == 0),
-                        stop=(a == passes[1] and t == 3),
+                        start=(opens and a == 0 and t == 0),
+                        stop=(a == 1 and t == 3),
                     )
+
+        def both_sums(b, operands, h):
+            for g in range(2):
+                own_passes(nb[g][b], operands, False)
+            clipped = tile([P, 4 * JB], F32, "clipped")
+            nc.scalar.activation(
+                clipped[:].rearrange("p (j t) -> p j t", t=4), nb[0][b][:].rearrange("p t j -> p j t"), mybir.ActivationFunctionType.Relu
+            )
+            nc.vector.tensor_tensor(
+                h.rearrange("p (j t) -> p j t", t=4),
+                nb[1][b][:].rearrange("p t j -> p j t"),
+                clipped[:].rearrange("p (j t) -> p j t", t=4),
+                ALU.max,
+            )
+
+        def own_add(b, operands, h_sum):
+            own = ps.tile([P, 4, JB], F32, name="own%d" % b, tag="bank%d" % b)
+            own_passes(own, operands, True)
             nc.vector.tensor_tensor(
                 h_sum.rearrange("p (j t) -> p j t", t=4),
                 own[:].rearrange("p t j -> p j t"),
@@ -229,39 +225,38 @@ def tile_list_pnet_res_kernel(
 
         g00 = interleave(c0_raw[:, :, 0:256], 256, "cg00", nc.scalar.copy)
         g01 = interleave(c0_raw[:, :, 256:512], 256, "cg01", nc.vector.tensor_copy)
+        copy_first(0)
+        q01 = quantise(g01, 256, "c01")
+        g10 = tile([P, 1024], BF16, "cg10")
+        round_into(g10[:, 0:512], c1_raw[0][:, :, 0:128], nc.vector.tensor_copy)
+        q00 = quantise(g00, 256, "c00")
         wc_codes = tile([P, 2, 2 * R], U8, "wc_codes")
         nc.vector.tensor_copy(
             wc_codes[:].bitcast(I32).rearrange("p a (t b e) -> p a t b e", t=4, e=2),
             wcw_raw[:].rearrange("p a (b t e) -> p a t b e", t=4, e=2),
         )
 
-        copy_first(0)
-        q01 = quantise(g01, 256, "c01")
-        q00 = quantise(g00, 256, "c00")
         copy_first(1)
         pool_max(0)
-        g10 = interleave(c1_raw[0], 256, "cg10", nc.scalar.copy)
+        round_into(g10[:, 512:1024], c1_raw[0][:, :, 128:256], nc.scalar.copy)
         copy_first(2)
-        pool_max(1)
         q10 = quantise(g10, 256, "c10")
+        pool_max(1)
         pool_max(2)
         g12 = interleave(c1_raw[1][:, :, 0:128], 128, "cg12", nc.scalar.copy)
         g13 = interleave(c1_raw[1][:, :, 128:256], 128, "cg13", nc.scalar.copy)
-        copy_first(3)
         wdg = interleave(wd_raw, N, "wdg", nc.scalar.copy)
-        sums = [tile([P, 4 * JB], BF16, "sum%d" % b) for b in range(4)]
+        sums = [tile([P, 4 * JB], BF16, "sum%d" % b) for b in range(3)]
         hs = [tile([P, 4 * JB], BF16, "h%d" % b) for b in range(4)]
-        own_add(0, [(q00, 0), (q10, 0)], sums[0][:])
         q12 = quantise(g12, 128, "c12")
-        own_add(1, [(q00, 128), (q10, 128)], sums[1][:])
         q13 = quantise(g13, 128, "c13")
-        pool_max(3)
+        own_add(0, [(q00, 0), (q10, 0)], sums[0][:])
+        own_add(1, [(q00, 128), (q10, 128)], sums[1][:])
         own_add(2, [(q01, 0), (q12, 0)], sums[2][:])
         wd_codes, wd_sc = quantise(wdg, N, "wd")
-        own_add(3, [(q01, 128), (q13, 0)], sums[3][:])
+        both_sums(3, [(q01, 128), (q13, 0)], hs[3][:])
         for b in range(3):
             nc.scalar.activation(hs[b][:], sums[b][:], mybir.ActivationFunctionType.Relu)
-        nc.vector.tensor_scalar_max(hs[3][:], sums[3][:], 0.0)
-        ys = [second(b, hs[b], JB) for b in range(4)]
-        for b in range(4):
+        ys = {b: second(b, hs[b], JB) for b in (0, 3, 1, 2)}
+        for b in ys:
             finish(b, ys[b], JB * b, JB)

@@ -14,9 +14,11 @@ U8 = mybir.dt.uint8
 FP8X4 = mybir.dt.float8_e4m3fn_x4
 FP4X4 = mybir.dt.float4_e2m1fn_x4
 ALU = mybir.AluOpType
+RELU = mybir.ActivationFunctionType.Relu
 
 P = 128
 JB = 128
+HALF = 256
 
 
 def tile_list_pnet_res_kernel(
@@ -27,25 +29,32 @@ def tile_list_pnet_res_kernel(
         sb = ctx.enter_context(tc.tile_pool(name="sb", bufs=1))
         ps = ctx.enter_context(tc.psum_pool(name="ps", bufs=1))
 
-        def tile(shape, dtype, name):
-            return sb.tile(shape, dtype, name=name, align_bytes=64)
+        def tile(shape, dtype, name, tag=None):
+            return sb.tile(shape, dtype, name=name, tag=tag or name, align_bytes=64)
+
+        def bank(shape, name, n):
+            return ps.tile(shape, F32, name=name, tag="bank%d" % n)
+
+        def rows4(x, a, h):
+            return x[512 * a : 512 * (a + 1), HALF * h : HALF * (h + 1)].rearrange("(p i) n -> p i n", i=4)
 
         offsets = sb.tile([P, 2 * J // 16], U16, name="offsets")
         nc.sync.dma_start(offsets[:], offs)
-        swin = sb.tile([P, T], U8, name="swin", tag="shared", align_bytes=64)
-        nc.sync.dma_start(swin[0:32, :].bitcast(I32), tab_scales.rearrange("a q t -> (a q) t").bitcast(I32))
-        twin = sb.tile([P, T], I32, name="twin", tag="words", align_bytes=64)
+        swin = tile([P, T], U8, "swin", "shared")
+        nc.sync.dma_start(swin[0:32, :].bitcast(I32), tab_scales.rearrange("a m t -> m a t").bitcast(I32))
+        twin = tile([P, T], I32, "twin", "words")
         nc.sync.dma_start(twin[:], tab_words[0].rearrange("p t b -> p (t b)").bitcast(I32))
-        w0_raw = tile([P, 4 * R], F32, "w0_raw")
-        nc.sync.dma_start(w0_raw[:], w[0:512, :].rearrange("(p i) r -> p (i r)", i=4))
+        w_raw = {}
+        for h in range(2):
+            w_raw[0, h] = tile([P, 4, HALF], F32, "w0_raw%d" % h)[:]
+            nc.sync.dma_start(w_raw[0, h], rows4(w, 0, h))
 
         wcs_raw = tile([P, 2, R], U8, "wcs_raw")
         nc.gpsimd.memset(wcs_raw[:].rearrange("p a r -> p (a r)").bitcast(I32), 0)
         nc.vector.memset(swin[32:64, :].bitcast(I32), 0)
         nc.vector.memset(swin[64:128, :].bitcast(I32), 0)
-        tplane = [tile([P, 2 * J], U8, "tplane%d" % a) for a in range(2)]
-        for a in range(2):
-            nc.vector.memset(tplane[a][:].bitcast(I32), 0)
+        tplane = tile([P, 4 * J], U8, "tplane")
+        nc.vector.memset(tplane[:].bitcast(I32), 0)
         for q in range(4):
             nc.gpsimd.dma_start(
                 wcs_raw[32 * q : 32 * q + 4, :, :].bitcast(I32),
@@ -54,158 +63,169 @@ def tile_list_pnet_res_kernel(
 
         sgot = tile([P, 2 * J], U8, "sgot")
         nc.vector.tensor_copy(sgot[:], swin[:].indirect(offsets[:]))
+        tgot = [tile([P, J], U32, "tgot%d" % g) for g in range(2)]
+        tcodes = [tile([P, 2, 2 * J], U8, "tcodes%d" % g) for g in range(2)]
+        for g in range(2):
+            nc.vector.tensor_copy(tgot[g][:], twin[:].bitcast(U32).indirect(offsets[:, 32 * g : 32 * (g + 1)]))
+        for g in range(2):
+            nc.vector.tensor_copy(tcodes[g][:].bitcast(U16), tgot[g][:].bitcast(U16).rearrange("p (j d) -> p d j", d=2))
 
-        tgot = sb.tile([P, 2 * J], U32, name="tgot", tag="got", align_bytes=64)
-        nc.vector.tensor_copy(tgot[:], twin[:].bitcast(U32).indirect(offsets[:]))
-        tcodes = tile([P, 2, 4 * J], U8, "tcodes")
-        nc.vector.tensor_copy(tcodes[:].bitcast(U16), tgot[:].bitcast(U16).rearrange("p (j d) -> p d j", d=2))
+        for q in range(4):
+            nc.sync.dma_start(tplane[32 * q : 32 * q + 4, :].bitcast(I32), sgot[8 * q : 8 * q + 8, :].bitcast(I32))
 
-        def move_plane(a, queue):
-            for q in range(4):
-                queue.dma_start(
-                    tplane[a][32 * q : 32 * q + 4, :].bitcast(I32),
-                    sgot[16 * a + 4 * q : 16 * a + 4 * q + 4, :].bitcast(I32),
-                )
+        late = tile([P, 8192], F32, "late", "shared")
 
-        late = sb.tile([P, 8192], F32, name="late", tag="shared", align_bytes=64)
-        move_plane(0, nc.sync)
-        w1_raw = late[:, 0:2048]
-        nc.sync.dma_start(w1_raw, w[512:1024, :].rearrange("(p i) r -> p (i r)", i=4))
-        move_plane(1, nc.sync)
-        w_raw = [w0_raw[:], w1_raw]
-        nc.sync.dma_start(late[:, 2048:4096], c[0:512, :].rearrange("(p i) j -> p (i j)", i=4))
-        c0_raw = late[:, 2048:4096].rearrange("p (i j) -> p i j", i=4)
-        c1_raw = [late[:, 4096 + 1024 * hf : 4096 + 1024 * (hf + 1)].rearrange("p (i j) -> p i j", i=4) for hf in range(2)]
-        nc.sync.dma_start(c1_raw[0], c[512:1024, 0:256].rearrange("(p i) j -> p i j", i=4))
-        wcw_raw = sb.tile([P, 2, R // 2], I32, name="wcw_raw", tag="words", align_bytes=64)
+        def piece(n):
+            return late[:, 1024 * n : 1024 * (n + 1)].rearrange("p (i n) -> p i n", i=4)
+
+        for h in range(2):
+            w_raw[1, h] = piece(h)
+            nc.sync.dma_start(w_raw[1, h], rows4(w, 1, h))
+        c_raw = {(h, a): piece(2 + 2 * h + a) for h in range(2) for a in range(2)}
+        nc.sync.dma_start(c_raw[0, 0], rows4(c, 0, 0))
+        wcw_raw = tile([P, 2, R // 2], I32, "wcw_raw", "words")
         nc.sync.dma_start(wcw_raw[:], wc_words.rearrange("a p b -> p a b").bitcast(I32))
-        nc.sync.dma_start(c1_raw[1], c[512:1024, 256:512].rearrange("(p i) j -> p i j", i=4))
-        wd_raw = late[:, 6144:7168].rearrange("p (i j) -> p i j", i=4)
+        nc.sync.dma_start(c_raw[0, 1], rows4(c, 1, 0))
+        nc.sync.dma_start(c_raw[1, 0], rows4(c, 0, 1))
+        last = {b: late[:, 512 * (b + 8) : 512 * (b + 9)].rearrange("p (i n) -> p i n", i=4) for b in (2, 3)}
+        for b in (3, 2):
+            nc.sync.dma_start(last[b], c[512:1024, JB * b : JB * (b + 1)].rearrange("(p i) n -> p i n", i=4))
+        wd_raw = piece(6)
         wd_v = wd.rearrange("(b t e) n -> t b e n", t=4, e=4)
         for t in range(4):
             nc.sync.dma_start(wd_raw[:, t, :], wd_v[t])
         res_sb = late[:, 7168:8192].rearrange("p (h j) -> p h j", h=2)
         nc.sync.dma_start(res_sb, res.rearrange("(h p) j -> p h j", h=2))
 
-        w_codes = [[tile([P, 2 * P], U32, "w_codes%d_%d" % (a, u)) for u in range(2)] for a in range(2)]
-        w_sc = [[tile([P, 2 * P], U8, "w_sc%d_%d" % (a, u)) for u in range(2)] for a in range(2)]
-        wg = [[sb.tile([P, 8 * P], BF16, name="wg%d_%d" % (a, u), tag="wg%d_%d" % (a, u), align_bytes=64) for u in range(2)] for a in range(2)]
+        wg = [tile([P, 16 * P], BF16, "wg%d" % a) for a in range(2)]
+        w_codes = [tile([P, 4 * P], U32, "w_codes%d" % a) for a in range(2)]
+        w_sc = [tile([P, 4 * P], U8, "w_sc%d" % a) for a in range(2)]
 
-        def cast_w(a, u, copy):
+        def round_w(a, h, ts, copy):
             copy(
-                wg[a][u][:].rearrange("p (t b e i) -> p t b i e", t=2, e=4, i=4),
-                w_raw[a].rearrange("p (i b t e) -> p t b i e", i=4, t=4, e=4)[:, 2 * u : 2 * u + 2],
+                wg[a][:].rearrange("p (t b e i) -> p t b i e", t=4, e=4, i=4)[:, ts, 16 * h : 16 * (h + 1)],
+                w_raw[a, h].rearrange("p i (b t e) -> p t b i e", t=4, e=4)[:, ts],
             )
 
         def quant_w(a, u):
-            nc.vector.quantize_mx(w_codes[a][u][:].bitcast(FP8X4), w_sc[a][u][:], wg[a][u][:])
+            nc.vector.quantize_mx(
+                w_codes[a][:, HALF * u : HALF * (u + 1)].bitcast(FP8X4),
+                w_sc[a][:, HALF * u : HALF * (u + 1)],
+                wg[a][:, 1024 * u : 1024 * (u + 1)],
+            )
 
-        cast_w(0, 0, nc.scalar.copy)
+        round_w(0, 0, slice(0, 4), nc.scalar.copy)
+        round_w(0, 1, slice(0, 4), nc.scalar.copy)
         quant_w(0, 0)
-        cast_w(0, 1, nc.scalar.copy)
         quant_w(0, 1)
-        cast_w(1, 0, nc.scalar.copy)
-        cast_w(1, 1, nc.vector.tensor_copy)
-        quant_w(1, 1)
-        quant_w(1, 0)
-        wc_sc = sb.tile([P, 2, R], U8, name="wc_sc", tag="wg1_0", align_bytes=64)
+        wc_sc = tile([P, 2, R], U8, "wc_sc", "wg0")
         nc.vector.tensor_copy(
             wc_sc[:].bitcast(I32).rearrange("p a (t b) -> p a t b", t=4),
             wcs_raw[:].bitcast(I32).rearrange("p a (b t) -> p a t b", t=4),
         )
+        round_w(1, 0, slice(0, 4), nc.scalar.copy)
+        round_w(1, 1, slice(0, 2), nc.vector.tensor_copy)
+        round_w(1, 1, slice(2, 4), nc.scalar.copy)
+        quant_w(1, 0)
+        quant_w(1, 1)
 
-        nb = [ [ps.tile([P, 4, JB], F32, name="nb%d_%d" % (g, b), tag="bank%d" % (4 * g + b)) for b in range(4)] for g in range(2)]
-        for a, b in [(0, 0), (0, 1), (0, 2), (1, 0), (1, 1), (1, 2), (1, 3), (0, 3)]:
-            if True:
+        nb = {}
+
+        def neighbours(b, a, opens, closes, halves=(0, 1)):
+            for u in halves:
                 for g in range(2):
-                    cols = slice(J * g + JB * b, J * g + JB * (b + 1))
-                    order = (2, 3, 0, 1) if a else (0, 1, 2, 3)
-                    opens = a == (1 if b == 3 else 0)
-                    for t in order:
-                        wcols = slice(P * (t % 2), P * (t % 2 + 1))
+                    for t in (2 * u, 2 * u + 1):
+                        j0 = JB * b
                         nc.tensor.matmul_mx(
-                            nb[g][b][:, t, :],
-                            lhsT=w_codes[a][t // 2][:, wcols].bitcast(FP8X4),
-                            lhsT_scale=w_sc[a][t // 2][:, wcols],
-                            rhs=tcodes[:, a, 2 * cols.start : 2 * cols.stop].bitcast(FP4X4),
-                            rhs_scale=tplane[a][:, cols],
-                            start=(opens and t == order[0]),
-                            stop=(b < 3 and not opens and t == order[3]),
+                            nb[g, b][:, t, :],
+                            lhsT=w_codes[a][:, P * t : P * (t + 1)].bitcast(FP8X4),
+                            lhsT_scale=w_sc[a][:, P * t : P * (t + 1)],
+                            rhs=tcodes[g][:, a, 2 * j0 : 2 * (j0 + JB)].bitcast(FP4X4),
+                            rhs_scale=tplane[:, 2 * J * a + J * g + j0 : 2 * J * a + J * g + j0 + JB],
+                            start=(opens and t == 0),
+                            stop=(closes and t == 3),
                         )
+
+        for b in range(3):
+            for g in range(2):
+                nb[g, b] = bank([P, 4, JB], "nb%d_%d" % (g, b), 4 * g + b)
+        neighbours(0, 0, True, False)
+        neighbours(1, 0, True, False, (0,))
+        neighbours(0, 1, False, True)
+        neighbours(1, 1, False, False)
+        neighbours(1, 0, False, True, (1,))
+        neighbours(2, 1, True, False)
+        neighbours(2, 0, False, True)
 
         def round_into(g, raw, copy):
             copy(g.rearrange("p (u v i) -> p u i v", v=4, i=4), raw.rearrange("p i (u v) -> p u i v", v=4))
 
-        def interleave(raw, width, name, copy):
-            g = sb.tile([P, 4 * width], BF16, name=name, tag=name, align_bytes=64)
-            round_into(g[:], raw, copy)
-            return g
-
         def quantise(g, width, name):
             codes = tile([P, width], U32, name + "_codes")
             scales = tile([P, width], U8, name + "_scales")
-            nc.vector.quantize_mx(codes[:].bitcast(FP8X4), scales[:], g[:])
+            nc.vector.quantize_mx(codes[:].bitcast(FP8X4), scales[:], g)
             return codes, scales
 
-        spent = [c0_raw[:, 0:2, 0:256], c0_raw[:, 2:4, 0:256]]
-        firsts = [x.rearrange("p u (j t) -> p u j t", t=4) for x in spent]
-        pooled = [tile([P, 4 * JB], F32, "pooled%d" % b) for b in range(3)]
+        def woven(x):
+            return x[:].rearrange("p t (u j) -> p u j t", u=4)
+
+        def spent(raw, g):
+            return raw[:, :, JB * g : JB * (g + 1)].rearrange("p u (j t) -> p u j t", t=4)
+
+        def fresh(name, dtype=F32, tag=None):
+            return tile([P, 4 * JB], dtype, name, tag)[:]
+
+        def runs(x):
+            return x.rearrange("p (u j t) -> p u j t", u=4, t=4)
+
+        cg = {(h, a): tile([P, 4 * HALF], BF16, "cg%d_%d" % (h, a)) for h in range(2) for a in range(2)}
+        cq = {}
+
+        def round_c(h, a, g, copy):
+            round_into(cg[h, a][:, 512 * g : 512 * (g + 1)], c_raw[h, a][:, :, JB * g : JB * (g + 1)], copy)
+
+        def quant_c(h, a):
+            cq[h, a] = quantise(cg[h, a][:], HALF, "c%d_%d" % (h, a))
+
+        def rows(raw, i, n):
+            return raw[:, i : i + n, :].rearrange("p i n -> p (i n)")
+
+        firsts = [runs(fresh("first0")), runs(fresh("first1")), runs(rows(c_raw[1, 0], 0, 2))]
+        pooled = [runs(rows(c_raw[0, 1], 0, 2)), runs(rows(c_raw[0, 1], 2, 2)), runs(fresh("pooled2"))]
 
         def copy_first(b):
-            if b == 2:
-                fresh = sb.tile([P, 2, 256], F32, name="first2", tag="cg00", align_bytes=64)
-                firsts.append(fresh[:].rearrange("p u (j t) -> p u j t", t=4))
-            nc.scalar.copy(firsts[b], nb[0][b][:].rearrange("p t (u j) -> p u j t", u=firsts[b].shape[1]))
+            nc.scalar.copy(firsts[b], woven(nb[0, b]))
 
         def pool_max(b):
-            nc.vector.tensor_tensor(
-                pooled[b][:].rearrange("p (u j t) -> p u j t", u=firsts[b].shape[1], t=4),
-                nb[1][b][:].rearrange("p t (u j) -> p u j t", u=firsts[b].shape[1]),
-                firsts[b],
-                ALU.max,
-            )
+            nc.vector.tensor_tensor(pooled[b], woven(nb[1, b]), firsts[b], ALU.max)
 
-        def own_passes(own, operands, opens):
-            for a in range(2):
-                (codes, scales), j0 = operands[a]
-                for t in range(4):
-                    nc.tensor.matmul_mx(
-                        own[:, t, :],
-                        lhsT=wc_codes[:, a, 2 * P * t : 2 * P * (t + 1)].bitcast(FP4X4),
-                        lhsT_scale=wc_sc[:, a, P * t : P * (t + 1)],
-                        rhs=codes[:, j0 : j0 + JB].bitcast(FP8X4),
-                        rhs_scale=scales[:, j0 : j0 + JB],
-                        start=(opens and a == 0 and t == 0),
-                        stop=(a == 1 and t == 3),
-                    )
+        def own_pass(dst, b, a, opens, closes):
+            codes, scales = cq[b // 2, a]
+            j0 = JB * (b % 2)
+            for t in range(4):
+                nc.tensor.matmul_mx(
+                    dst[:, t, :],
+                    lhsT=wc_codes[:, a, 2 * P * t : 2 * P * (t + 1)].bitcast(FP4X4),
+                    lhsT_scale=wc_sc[:, a, P * t : P * (t + 1)],
+                    rhs=codes[:, j0 : j0 + JB].bitcast(FP8X4),
+                    rhs_scale=scales[:, j0 : j0 + JB],
+                    start=(opens and t == 0),
+                    stop=(closes and t == 3),
+                )
 
-        def both_sums(b, operands, h):
-            for g in range(2):
-                own_passes(nb[g][b], operands, False)
-            clipped = tile([P, 4 * JB], F32, "clipped")
-            nc.scalar.activation(
-                clipped[:].rearrange("p (j t) -> p j t", t=4), nb[0][b][:].rearrange("p t j -> p j t"), mybir.ActivationFunctionType.Relu
-            )
-            nc.vector.tensor_tensor(
-                h.rearrange("p (j t) -> p j t", t=4),
-                nb[1][b][:].rearrange("p t j -> p j t"),
-                clipped[:].rearrange("p (j t) -> p j t", t=4),
-                ALU.max,
-            )
+        sums = [rows(last[3], 0, 2).bitcast(BF16), rows(last[2], 0, 2).bitcast(BF16), rows(wd_raw, 2, 1).bitcast(BF16)]
 
-        def own_add(b, operands, h_sum):
-            own = ps.tile([P, 4, JB], F32, name="own%d" % b, tag="bank%d" % b)
-            own_passes(own, operands, True)
-            nc.vector.tensor_tensor(
-                h_sum.rearrange("p (j t) -> p j t", t=4),
-                own[:].rearrange("p t j -> p j t"),
-                pooled[b][:].rearrange("p (j t) -> p j t", t=4),
-                ALU.add,
-            )
+        def own_add(b):
+            nc.vector.tensor_tensor(runs(sums[b]), woven(own[b]), pooled[b], ALU.add)
 
-        def second(n, h, width):
-            codes, scales = quantise(h, width, "h%d" % n)
-            y = ps.tile([P, 2, width], F32, name="y%d" % n, tag="bank%d" % (4 + n))
+        hq = {}
+
+        def relu(b, h):
+            nc.vector.tensor_scalar_max(h, sums[b], 0.0)
+
+        def second(b, n):
+            codes, scales = hq[b]
+            y = bank([P, 2, JB], "y%d" % b, n)
             for nh in range(2):
                 nc.tensor.matmul_mx(
                     y[:, nh, :],
@@ -218,45 +238,66 @@ def tile_list_pnet_res_kernel(
                 )
             return y
 
-        def finish(n, y, j0, width):
-            o = tile([P, 2, width], F32, "o%d" % n)
-            nc.vector.tensor_tensor(o[:], y[:], res_sb[:, :, j0 : j0 + width], ALU.add)
-            nc.sync.dma_start(out.rearrange("(h p) j -> p h j", h=2)[:, :, j0 : j0 + width], o[:])
+        def finish(b, y, nhs):
+            o = tile([P, nhs.stop - nhs.start, JB], F32, "o%d_%d" % (b, nhs.start))
+            nc.vector.tensor_tensor(o[:], y[:, nhs, :], res_sb[:, nhs, JB * b : JB * (b + 1)], ALU.add)
+            nc.sync.dma_start(out.rearrange("(h p) j -> p h j", h=2)[:, nhs, JB * b : JB * (b + 1)], o[:])
 
-        g00 = interleave(c0_raw[:, :, 0:256], 256, "cg00", nc.scalar.copy)
-        g01 = interleave(c0_raw[:, :, 256:512], 256, "cg01", nc.vector.tensor_copy)
-        copy_first(0)
-        q01 = quantise(g01, 256, "c01")
-        g10 = tile([P, 1024], BF16, "cg10")
-        round_into(g10[:, 0:512], c1_raw[0][:, :, 0:128], nc.vector.tensor_copy)
-        q00 = quantise(g00, 256, "c00")
+        round_into(cg[0, 0][:], c_raw[0, 0], nc.scalar.copy)
         wc_codes = tile([P, 2, 2 * R], U8, "wc_codes")
         nc.vector.tensor_copy(
             wc_codes[:].bitcast(I32).rearrange("p a (t b e) -> p a t b e", t=4, e=2),
             wcw_raw[:].rearrange("p a (b t e) -> p a t b e", t=4, e=2),
         )
-
-        copy_first(1)
+        quant_c(0, 0)
+        round_into(cg[0, 1][:], c_raw[0, 1], nc.vector.tensor_copy)
+        copy_first(0)
         pool_max(0)
-        round_into(g10[:, 512:1024], c1_raw[0][:, :, 128:256], nc.scalar.copy)
-        copy_first(2)
-        q10 = quantise(g10, 256, "c10")
+        quant_c(0, 1)
+        copy_first(1)
+        own = [bank([P, 4, JB], "own0", 3), bank([P, 4, JB], "own1", 7)]
+        for a in range(2):
+            for b in range(2):
+                own_pass(own[b], b, a, a == 0, a == 1)
         pool_max(1)
+        for g in range(2):
+            nb[g, 3] = bank([P, 4, JB], "nb%d_3" % g, 4 * g + 1)
+        neighbours(3, 1, True, False)
+        neighbours(3, 0, False, False)
+
+        round_into(cg[1, 0][:], c_raw[1, 0], nc.scalar.copy)
+        round_into(cg[1, 1][:, 512:1024], last[3], nc.vector.tensor_copy)
+        quant_c(1, 0)
+        own_add(0)
+        round_into(cg[1, 1][:, 0:512], last[2], nc.scalar.copy)
+        quant_c(1, 1)
+        own_add(1)
+        copy_first(2)
         pool_max(2)
-        g12 = interleave(c1_raw[1][:, :, 0:128], 128, "cg12", nc.scalar.copy)
-        g13 = interleave(c1_raw[1][:, :, 128:256], 128, "cg13", nc.scalar.copy)
-        wdg = interleave(wd_raw, N, "wdg", nc.scalar.copy)
-        sums = [tile([P, 4 * JB], BF16, "sum%d" % b) for b in range(3)]
-        hs = [tile([P, 4 * JB], BF16, "h%d" % b) for b in range(4)]
-        q12 = quantise(g12, 128, "c12")
-        q13 = quantise(g13, 128, "c13")
-        own_add(0, [(q00, 0), (q10, 0)], sums[0][:])
-        own_add(1, [(q00, 128), (q10, 128)], sums[1][:])
-        own_add(2, [(q01, 0), (q12, 0)], sums[2][:])
-        wd_codes, wd_sc = quantise(wdg, N, "wd")
-        both_sums(3, [(q01, 128), (q13, 0)], hs[3][:])
-        for b in range(3):
-            nc.scalar.activation(hs[b][:], sums[b][:], mybir.ActivationFunctionType.Relu)
-        ys = {b: second(b, hs[b], JB) for b in (0, 3, 1, 2)}
-        for b in ys:
-            finish(b, ys[b], JB * b, JB)
+        hs = [fresh("h%d" % b, BF16) for b in range(4)]
+        nc.scalar.activation(hs[0], sums[0], RELU)
+        relu(1, hs[1])
+        for b in range(2):
+            hq[b] = quantise(hs[b], JB, "h%d" % b)
+        own.append(bank([P, 4, JB], "own2", 0))
+        for a in range(2):
+            own_pass(own[2], 2, a, a == 0, a == 1)
+            for g in range(2):
+                own_pass(nb[g, 3], 3, a, False, a == 1)
+        wdg = tile([P, 4 * N], BF16, "wdg")
+        round_into(wdg[:], wd_raw, nc.scalar.copy)
+        wd_codes, wd_sc = quantise(wdg[:], N, "wd")
+        ys = {b: second(b, n) for b, n in ((0, 4), (1, 3))}
+        own_add(2)
+        clipped = runs(rows(wd_raw, 0, 2))
+        nc.scalar.activation(clipped, woven(nb[0, 3]), RELU)
+        nc.vector.tensor_tensor(runs(hs[3]), woven(nb[1, 3]), clipped, ALU.max)
+        nc.scalar.activation(hs[2], sums[2], RELU)
+        finish(0, ys[0], slice(0, 2))
+        for b, n in ((3, 6), (2, 7)):
+            hq[b] = quantise(hs[b], JB, "h%d" % b)
+            ys[b] = second(b, n)
+        for b in (1, 3):
+            finish(b, ys[b], slice(0, 2))
+        for nh in range(2):
+            finish(2, ys[2], slice(nh, nh + 1))

@@ -41,7 +41,7 @@ def tile_list_pnet_res_kernel(
         offsets = sb.tile([P, 2 * J // 16], U16, name="offsets")
         nc.sync.dma_start(offsets[:], offs)
         swin = tile([P, T], U8, "swin", "shared")
-        nc.sync.dma_start(swin[0:32, :].bitcast(I32), tab_scales.rearrange("a m t -> m a t").bitcast(I32))
+        nc.sync.dma_start(swin[96:128, :].bitcast(I32), tab_scales.rearrange("a m t -> m a t").bitcast(I32))
         twin = tile([P, T], I32, "twin", "words")
         nc.sync.dma_start(twin[:], tab_words[0].rearrange("p t b -> p (t b)").bitcast(I32))
         w_raw = {}
@@ -51,8 +51,7 @@ def tile_list_pnet_res_kernel(
 
         wcs_raw = tile([P, 2, R], U8, "wcs_raw")
         nc.gpsimd.memset(wcs_raw[:].rearrange("p a r -> p (a r)").bitcast(I32), 0)
-        nc.vector.memset(swin[32:64, :].bitcast(I32), 0)
-        nc.vector.memset(swin[64:128, :].bitcast(I32), 0)
+        nc.vector.memset(swin[0:96, :].bitcast(I32), 0)
         tplane = tile([P, 4 * J], U8, "tplane")
         nc.vector.memset(tplane[:].bitcast(I32), 0)
         for q in range(4):
@@ -67,11 +66,32 @@ def tile_list_pnet_res_kernel(
         tcodes = [tile([P, 2, 2 * J], U8, "tcodes%d" % g) for g in range(2)]
         for g in range(2):
             nc.vector.tensor_copy(tgot[g][:], twin[:].bitcast(U32).indirect(offsets[:, 32 * g : 32 * (g + 1)]))
+        zeros = tile([P, 2 * J], BF16, "zeros")
+        nc.vector.memset(zeros[:].bitcast(I32), 0)
+        z_codes = tile([P, J], U32, "z_codes")
+        z_sc = tile([P, J], U8, "z_sc")
+        for h in range(2):
+            cols = slice(HALF * h, HALF * (h + 1))
+            nc.vector.quantize_mx(z_codes[:, cols].bitcast(FP8X4), z_sc[:, cols], zeros[:])
+        x_codes = tile([P, 32], U32, "x_codes", "words")
+        x_sc = tile([P, 32], U8, "x_sc")
+        nc.vector.quantize_mx(x_codes[:].bitcast(FP8X4), x_sc[:], zeros[:, 0:128])
+        idle = bank([P, J], "idle", 3)
+        for n in range(2):
+            nc.tensor.matmul_mx(
+                idle[0:32, :],
+                lhsT=x_codes[:].bitcast(FP8X4),
+                lhsT_scale=x_sc[:],
+                rhs=z_codes[:].bitcast(FP8X4),
+                rhs_scale=z_sc[:],
+                start=True,
+                stop=True,
+            )
         for g in range(2):
             nc.vector.tensor_copy(tcodes[g][:].bitcast(U16), tgot[g][:].bitcast(U16).rearrange("p (j d) -> p d j", d=2))
 
         for q in range(4):
-            nc.sync.dma_start(tplane[32 * q : 32 * q + 4, :].bitcast(I32), sgot[8 * q : 8 * q + 8, :].bitcast(I32))
+            nc.sync.dma_start(tplane[32 * q : 32 * q + 4, :].bitcast(I32), sgot[96 + 8 * q : 96 + 8 * q + 8, :].bitcast(I32))
 
         late = tile([P, 8192], F32, "late", "shared")
 
@@ -83,7 +103,7 @@ def tile_list_pnet_res_kernel(
             nc.sync.dma_start(w_raw[1, h], rows4(w, 1, h))
         c_raw = {(h, a): piece(2 + 2 * h + a) for h in range(2) for a in range(2)}
         nc.sync.dma_start(c_raw[0, 0], rows4(c, 0, 0))
-        wcw_raw = tile([P, 2, R // 2], I32, "wcw_raw", "words")
+        wcw_raw = tile([P, 2, R // 2], I32, "wcw_raw")
         nc.sync.dma_start(wcw_raw[:], wc_words.rearrange("a p b -> p a b").bitcast(I32))
         nc.sync.dma_start(c_raw[0, 1], rows4(c, 1, 0))
         nc.sync.dma_start(c_raw[1, 0], rows4(c, 0, 1))

@@ -87,8 +87,12 @@ def tile_list_pnet_res_kernel(
                 start=True,
                 stop=True,
             )
-        for g in range(2):
-            nc.vector.tensor_copy(tcodes[g][:].bitcast(U16), tgot[g][:].bitcast(U16).rearrange("p (j d) -> p d j", d=2))
+
+        def part(g, a):
+            nc.vector.tensor_copy(tcodes[g][:, a, :].bitcast(U16), tgot[g][:].bitcast(U16).rearrange("p (j d) -> p d j", d=2)[:, a, :])
+
+        part(0, 0)
+        part(1, 0)
 
         for q in range(4):
             nc.sync.dma_start(tplane[32 * q : 32 * q + 4, :].bitcast(I32), sgot[96 + 8 * q : 96 + 8 * q + 8, :].bitcast(I32))
@@ -135,9 +139,12 @@ def tile_list_pnet_res_kernel(
             )
 
         round_w(0, 0, slice(0, 4), nc.scalar.copy)
-        round_w(0, 1, slice(0, 4), nc.scalar.copy)
+        round_w(0, 1, slice(0, 2), nc.scalar.copy)
+        round_w(0, 1, slice(2, 4), nc.scalar.copy)
         quant_w(0, 0)
+        part(0, 1)
         quant_w(0, 1)
+        part(1, 1)
         wc_sc = tile([P, 2, R], U8, "wc_sc", "wg0")
         nc.vector.tensor_copy(
             wc_sc[:].bitcast(I32).rearrange("p a (t b) -> p a t b", t=4),
@@ -169,11 +176,11 @@ def tile_list_pnet_res_kernel(
         for b in range(3):
             for g in range(2):
                 nb[g, b] = bank([P, 4, JB], "nb%d_%d" % (g, b), 4 * g + b)
-        neighbours(0, 0, True, False)
-        neighbours(1, 0, True, False, (0,))
+        for u in range(2):
+            for b in range(2):
+                neighbours(b, 0, True, False, (u,))
         neighbours(0, 1, False, True)
-        neighbours(1, 1, False, False)
-        neighbours(1, 0, False, True, (1,))
+        neighbours(1, 1, False, True)
         neighbours(2, 1, True, False)
         neighbours(2, 0, False, True)
 
@@ -301,9 +308,9 @@ def tile_list_pnet_res_kernel(
             hq[b] = quantise(hs[b], JB, "h%d" % b)
         own.append(bank([P, 4, JB], "own2", 0))
         for a in range(2):
+            own_pass(nb[0, 3], 3, a, False, a == 1)
             own_pass(own[2], 2, a, a == 0, a == 1)
-            for g in range(2):
-                own_pass(nb[g, 3], 3, a, False, a == 1)
+            own_pass(nb[1, 3], 3, a, False, a == 1)
         wdg = tile([P, 4 * N], BF16, "wdg")
         round_into(wdg[:], wd_raw, nc.scalar.copy)
         wd_codes, wd_sc = quantise(wdg[:], N, "wd")

@@ -106,10 +106,10 @@ def tile_list_pnet_res_kernel(
             w_raw[1, h] = piece(h)
             nc.sync.dma_start(w_raw[1, h], rows4(w, 1, h))
         c_raw = {(h, a): piece(2 + 2 * h + a) for h in range(2) for a in range(2)}
-        nc.sync.dma_start(c_raw[0, 0], rows4(c, 0, 0))
+        for a in range(2):
+            nc.sync.dma_start(c_raw[0, a], rows4(c, a, 0))
         wcw_raw = tile([P, 2, R // 2], I32, "wcw_raw")
         nc.sync.dma_start(wcw_raw[:], wc_words.rearrange("a p b -> p a b").bitcast(I32))
-        nc.sync.dma_start(c_raw[0, 1], rows4(c, 1, 0))
         nc.sync.dma_start(c_raw[1, 0], rows4(c, 0, 1))
         last = {b: late[:, 512 * (b + 8) : 512 * (b + 9)].rearrange("p (i n) -> p i n", i=4) for b in (2, 3)}
         for b in (3, 2):
@@ -271,16 +271,16 @@ def tile_list_pnet_res_kernel(
             nc.sync.dma_start(out.rearrange("(h p) j -> p h j", h=2)[:, nhs, JB * b : JB * (b + 1)], o[:])
 
         round_into(cg[0, 0][:], c_raw[0, 0], nc.scalar.copy)
+        round_into(cg[0, 1][:], c_raw[0, 1], nc.vector.tensor_copy)
+        quant_c(0, 0)
         wc_codes = tile([P, 2, 2 * R], U8, "wc_codes")
         nc.vector.tensor_copy(
             wc_codes[:].bitcast(I32).rearrange("p a (t b e) -> p a t b e", t=4, e=2),
             wcw_raw[:].rearrange("p a (b t e) -> p a t b e", t=4, e=2),
         )
-        quant_c(0, 0)
-        round_into(cg[0, 1][:], c_raw[0, 1], nc.vector.tensor_copy)
+        quant_c(0, 1)
         copy_first(0)
         pool_max(0)
-        quant_c(0, 1)
         copy_first(1)
         own = [bank([P, 4, JB], "own0", 3), bank([P, 4, JB], "own1", 7)]
         for a in range(2):
@@ -288,7 +288,7 @@ def tile_list_pnet_res_kernel(
                 own_pass(own[b], b, a, a == 0, a == 1)
         pool_max(1)
         for g in range(2):
-            nb[g, 3] = bank([P, 4, JB], "nb%d_3" % g, 4 * g + 1)
+            nb[g, 3] = bank([P, 4, JB], "nb%d_3" % g, 4 * g)
         neighbours(3, 1, True, False)
         neighbours(3, 0, False, False)
 
@@ -306,7 +306,7 @@ def tile_list_pnet_res_kernel(
         relu(1, hs[1])
         for b in range(2):
             hq[b] = quantise(hs[b], JB, "h%d" % b)
-        own.append(bank([P, 4, JB], "own2", 0))
+        own.append(bank([P, 4, JB], "own2", 1))
         for a in range(2):
             own_pass(nb[0, 3], 3, a, False, a == 1)
             own_pass(own[2], 2, a, a == 0, a == 1)
@@ -314,7 +314,7 @@ def tile_list_pnet_res_kernel(
         wdg = tile([P, 4 * N], BF16, "wdg")
         round_into(wdg[:], wd_raw, nc.scalar.copy)
         wd_codes, wd_sc = quantise(wdg[:], N, "wd")
-        ys = {b: second(b, n) for b, n in ((0, 4), (1, 3))}
+        ys = {b: second(b, n) for b, n in ((0, 5), (1, 3))}
         own_add(2)
         clipped = runs(rows(wd_raw, 0, 2))
         nc.scalar.activation(clipped, woven(nb[0, 3]), RELU)

from contextlib import ExitStack

import concourse.mybir as mybir

K, R, N, T, J = 1024, 512, 256, 4096, 512
FLOPS = 2 * K * R * J * 3 + 2 * R * N * J

F32 = mybir.dt.float32
BF16 = mybir.dt.bfloat16
I32 = mybir.dt.int32
U32 = mybir.dt.uint32
U16 = mybir.dt.uint16
U8 = mybir.dt.uint8
FP8X4 = mybir.dt.float8_e4m3fn_x4
FP4X4 = mybir.dt.float4_e2m1fn_x4
ALU = mybir.AluOpType
RELU = mybir.ActivationFunctionType.Relu

P = 128
JB = 128
HALF = 256


def tile_list_pnet_res_kernel(
    tc, tab_words, tab_scales, c, w, wc_words, wc_scales, wd, res, offs, out
):
    nc = tc.nc
    with ExitStack() as ctx:
        sb = ctx.enter_context(tc.tile_pool(name="sb", bufs=1))
        ps = ctx.enter_context(tc.psum_pool(name="ps", bufs=1))

        def tile(shape, dtype, name, tag=None):
            return sb.tile(shape, dtype, name=name, tag=tag or name, align_bytes=64)

        def bank(shape, name, n):
            return ps.tile(shape, F32, name=name, tag="bank%d" % n)

        def rows4(x, a, h):
            return x[512 * a : 512 * (a + 1), HALF * h : HALF * (h + 1)].rearrange("(p i) n -> p i n", i=4)

        offsets = sb.tile([P, 2 * J // 16], U16, name="offsets")
        nc.sync.dma_start(offsets[:], offs)
        swin = tile([P, T], U8, "swin", "shared")
        nc.sync.dma_start(swin[96:128, :].bitcast(I32), tab_scales.rearrange("a m t -> m a t").bitcast(I32))
        twin = tile([P, T], I32, "twin", "words")
        nc.sync.dma_start(twin[:], tab_words[0].rearrange("p t b -> p (t b)").bitcast(I32))
        w_raw = {}
        for h in range(2):
            w_raw[0, h] = tile([P, 4, HALF], F32, "w0_raw%d" % h)[:]
            nc.sync.dma_start(w_raw[0, h], rows4(w, 0, h))

        wcs_raw = tile([P, 2, R], U8, "wcs_raw")
        nc.gpsimd.memset(wcs_raw[:].rearrange("p a r -> p (a r)").bitcast(I32), 0)
        nc.vector.memset(swin[0:96, :].bitcast(I32), 0)
        tplane = tile([P, 4 * J], U8, "tplane")
        nc.vector.memset(tplane[:].bitcast(I32), 0)
        for q in range(4):
            nc.gpsimd.dma_start(
                wcs_raw[32 * q : 32 * q + 4, :, :].bitcast(I32),
                wc_scales[:, 4 * q : 4 * q + 4, :].rearrange("a s r -> s a r").bitcast(I32),
            )

        sgot = tile([P, 2 * J], U8, "sgot")
        nc.vector.tensor_copy(sgot[:], swin[:].indirect(offsets[:]))
        tgot = [tile([P, J], U32, "tgot%d" % g) for g in range(2)]
        tcodes = [tile([P, 2, 2 * J], U8, "tcodes%d" % g) for g in range(2)]
        for g in range(2):
            nc.vector.tensor_copy(tgot[g][:], twin[:].bitcast(U32).indirect(offsets[:, 32 * g : 32 * (g + 1)]))
        zeros = tile([P, 2 * J], BF16, "zeros")
        nc.vector.memset(zeros[:].bitcast(I32), 0)
        z_codes = tile([P, J], U32, "z_codes")
        z_sc = tile([P, J], U8, "z_sc")
        for h in range(2):
            cols = slice(HALF * h, HALF * (h + 1))
            nc.vector.quantize_mx(z_codes[:, cols].bitcast(FP8X4), z_sc[:, cols], zeros[:])
        x_codes = tile([P, 32], U32, "x_codes", "words")
        x_sc = tile([P, 32], U8, "x_sc")
        nc.vector.quantize_mx(x_codes[:].bitcast(FP8X4), x_sc[:], zeros[:, 0:128])
        idle = bank([P, J], "idle", 3)
        for n in range(2):
            nc.tensor.matmul_mx(
                idle[0:32, :],
                lhsT=x_codes[:].bitcast(FP8X4),
                lhsT_scale=x_sc[:],
                rhs=z_codes[:].bitcast(FP8X4),
                rhs_scale=z_sc[:],
                start=True,
                stop=True,
            )

        def part(g, a):
            nc.vector.tensor_copy(tcodes[g][:, a, :].bitcast(U16), tgot[g][:].bitcast(U16).rearrange("p (j d) -> p d j", d=2)[:, a, :])

        part(0, 0)
        part(1, 0)

        for q in range(4):
            nc.sync.dma_start(tplane[32 * q : 32 * q + 4, :].bitcast(I32), sgot[96 + 8 * q : 96 + 8 * q + 8, :].bitcast(I32))

        late = tile([P, 8192], F32, "late", "shared")

        def piece(n):
            return late[:, 1024 * n : 1024 * (n + 1)].rearrange("p (i n) -> p i n", i=4)

        for h in range(2):
            w_raw[1, h] = piece(h)
            nc.sync.dma_start(w_raw[1, h], rows4(w, 1, h))
        c_raw = {(h, a): piece(2 + 2 * h + a) for h in range(2) for a in range(2)}
        for a in range(2):
            nc.sync.dma_start(c_raw[0, a], rows4(c, a, 0))
        wcw_raw = tile([P, 2, R // 2], I32, "wcw_raw")
        nc.sync.dma_start(wcw_raw[:], wc_words.rearrange("a p b -> p a b").bitcast(I32))
        nc.sync.dma_start(c_raw[1, 0], rows4(c, 0, 1))
        last = {b: late[:, 512 * (b + 8) : 512 * (b + 9)].rearrange("p (i n) -> p i n", i=4) for b in (2, 3)}
        for b in (3, 2):
            nc.sync.dma_start(last[b], c[512:1024, JB * b : JB * (b + 1)].rearrange("(p i) n -> p i n", i=4))
        wd_raw = piece(6)
        wd_v = wd.rearrange("(b t e) n -> t b e n", t=4, e=4)
        for t in range(4):
            nc.sync.dma_start(wd_raw[:, t, :], wd_v[t])
        res_sb = late[:, 7168:8192].rearrange("p (h j) -> p h j", h=2)
        nc.sync.dma_start(res_sb, res.rearrange("(h p) j -> p h j", h=2))

        wg = [tile([P, 16 * P], BF16, "wg%d" % a) for a in range(2)]
        w_codes = [tile([P, 4 * P], U32, "w_codes%d" % a) for a in range(2)]
        w_sc = [tile([P, 4 * P], U8, "w_sc%d" % a) for a in range(2)]

        def round_w(a, h, ts, copy):
            copy(
                wg[a][:].rearrange("p (t b e i) -> p t b i e", t=4, e=4, i=4)[:, ts, 16 * h : 16 * (h + 1)],
                w_raw[a, h].rearrange("p i (b t e) -> p t b i e", t=4, e=4)[:, ts],
            )

        def quant_w(a, u):
            nc.vector.quantize_mx(
                w_codes[a][:, HALF * u : HALF * (u + 1)].bitcast(FP8X4),
                w_sc[a][:, HALF * u : HALF * (u + 1)],
                wg[a][:, 1024 * u : 1024 * (u + 1)],
            )

        round_w(0, 0, slice(0, 4), nc.scalar.copy)
        round_w(0, 1, slice(0, 2), nc.scalar.copy)
        round_w(0, 1, slice(2, 4), nc.scalar.copy)
        quant_w(0, 0)
        part(0, 1)
        quant_w(0, 1)
        part(1, 1)
        wc_sc = tile([P, 2, R], U8, "wc_sc", "wg0")
        nc.vector.tensor_copy(
            wc_sc[:].bitcast(I32).rearrange("p a (t b) -> p a t b", t=4),
            wcs_raw[:].bitcast(I32).rearrange("p a (b t) -> p a t b", t=4),
        )
        round_w(1, 0, slice(0, 4), nc.scalar.copy)
        round_w(1, 1, slice(0, 2), nc.vector.tensor_copy)
        round_w(1, 1, slice(2, 4), nc.scalar.copy)
        quant_w(1, 0)
        quant_w(1, 1)

        nb = {}

        def neighbours(b, a, opens, closes, halves=(0, 1)):
            for u in halves:
                for g in range(2):
                    for t in (2 * u, 2 * u + 1):
                        j0 = JB * b
                        nc.tensor.matmul_mx(
                            nb[g, b][:, t, :],
                            lhsT=w_codes[a][:, P * t : P * (t + 1)].bitcast(FP8X4),
                            lhsT_scale=w_sc[a][:, P * t : P * (t + 1)],
                            rhs=tcodes[g][:, a, 2 * j0 : 2 * (j0 + JB)].bitcast(FP4X4),
                            rhs_scale=tplane[:, 2 * J * a + J * g + j0 : 2 * J * a + J * g + j0 + JB],
                            start=(opens and t == 0),
                            stop=(closes and t == 3),
                        )

        for b in range(3):
            for g in range(2):
                nb[g, b] = bank([P, 4, JB], "nb%d_%d" % (g, b), 4 * g + b)
        for u in range(2):
            for b in range(2):
                neighbours(b, 0, True, False, (u,))
        neighbours(0, 1, False, True)
        neighbours(1, 1, False, True)
        neighbours(2, 1, True, False)
        neighbours(2, 0, False, True)

        def round_into(g, raw, copy):
            copy(g.rearrange("p (u v i) -> p u i v", v=4, i=4), raw.rearrange("p i (u v) -> p u i v", v=4))

        def quantise(g, width, name):
            codes = tile([P, width], U32, name + "_codes")
            scales = tile([P, width], U8, name + "_scales")
            nc.vector.quantize_mx(codes[:].bitcast(FP8X4), scales[:], g)
            return codes, scales

        def woven(x):
            return x[:].rearrange("p t (u j) -> p u j t", u=4)

        def spent(raw, g):
            return raw[:, :, JB * g : JB * (g + 1)].rearrange("p u (j t) -> p u j t", t=4)

        def fresh(name, dtype=F32, tag=None):
            return tile([P, 4 * JB], dtype, name, tag)[:]

        def runs(x):
            return x.rearrange("p (u j t) -> p u j t", u=4, t=4)

        cg = {(h, a): tile([P, 4 * HALF], BF16, "cg%d_%d" % (h, a)) for h in range(2) for a in range(2)}
        cq = {}

        def round_c(h, a, g, copy):
            round_into(cg[h, a][:, 512 * g : 512 * (g + 1)], c_raw[h, a][:, :, JB * g : JB * (g + 1)], copy)

        def quant_c(h, a):
            cq[h, a] = quantise(cg[h, a][:], HALF, "c%d_%d" % (h, a))

        def rows(raw, i, n):
            return raw[:, i : i + n, :].rearrange("p i n -> p (i n)")

        firsts = [runs(fresh("first0")), runs(fresh("first1")), runs(rows(c_raw[1, 0], 0, 2))]
        pooled = [runs(rows(c_raw[0, 1], 0, 2)), runs(rows(c_raw[0, 1], 2, 2)), runs(fresh("pooled2"))]

        def copy_first(b):
            nc.scalar.copy(firsts[b], woven(nb[0, b]))

        def pool_max(b):
            nc.vector.tensor_tensor(pooled[b], woven(nb[1, b]), firsts[b], ALU.max)

        def own_pass(dst, b, a, opens, closes):
            codes, scales = cq[b // 2, a]
            j0 = JB * (b % 2)
            for t in range(4):
                nc.tensor.matmul_mx(
                    dst[:, t, :],
                    lhsT=wc_codes[:, a, 2 * P * t : 2 * P * (t + 1)].bitcast(FP4X4),
                    lhsT_scale=wc_sc[:, a, P * t : P * (t + 1)],
                    rhs=codes[:, j0 : j0 + JB].bitcast(FP8X4),
                    rhs_scale=scales[:, j0 : j0 + JB],
                    start=(opens and t == 0),
                    stop=(closes and t == 3),
                )

        sums = [rows(last[3], 0, 2).bitcast(BF16), rows(last[2], 0, 2).bitcast(BF16), rows(wd_raw, 2, 1).bitcast(BF16)]

        def own_add(b):
            nc.vector.tensor_tensor(runs(sums[b]), woven(own[b]), pooled[b], ALU.add)

        hq = {}

        def relu(b, h):
            nc.vector.tensor_scalar_max(h, sums[b], 0.0)

        def second(b, n):
            codes, scales = hq[b]
            y = bank([P, 2, JB], "y%d" % b, n)
            for nh in range(2):
                nc.tensor.matmul_mx(
                    y[:, nh, :],
                    lhsT=wd_codes[:, P * nh : P * (nh + 1)].bitcast(FP8X4),
                    lhsT_scale=wd_sc[:, P * nh : P * (nh + 1)],
                    rhs=codes[:].bitcast(FP8X4),
                    rhs_scale=scales[:],
                    start=True,
                    stop=True,
                )
            return y

        def finish(b, y, nhs):
            o = tile([P, nhs.stop - nhs.start, JB], F32, "o%d_%d" % (b, nhs.start))
            nc.vector.tensor_tensor(o[:], y[:, nhs, :], res_sb[:, nhs, JB * b : JB * (b + 1)], ALU.add)
            nc.sync.dma_start(out.rearrange("(h p) j -> p h j", h=2)[:, nhs, JB * b : JB * (b + 1)], o[:])

        round_into(cg[0, 0][:], c_raw[0, 0], nc.scalar.copy)
        round_into(cg[0, 1][:], c_raw[0, 1], nc.vector.tensor_copy)
        quant_c(0, 0)
        wc_codes = tile([P, 2, 2 * R], U8, "wc_codes")
        nc.vector.tensor_copy(
            wc_codes[:].bitcast(I32).rearrange("p a (t b e) -> p a t b e", t=4, e=2),
            wcw_raw[:].rearrange("p a (b t e) -> p a t b e", t=4, e=2),
        )
        quant_c(0, 1)
        copy_first(0)
        pool_max(0)
        copy_first(1)
        own = [bank([P, 4, JB], "own0", 3), bank([P, 4, JB], "own1", 7)]
        for a in range(2):
            for b in range(2):
                own_pass(own[b], b, a, a == 0, a == 1)
        pool_max(1)
        for g in range(2):
            nb[g, 3] = bank([P, 4, JB], "nb%d_3" % g, 4 * g)
        neighbours(3, 1, True, False)
        neighbours(3, 0, False, False)

        round_into(cg[1, 0][:], c_raw[1, 0], nc.scalar.copy)
        round_into(cg[1, 1][:, 512:1024], last[3], nc.vector.tensor_copy)
        quant_c(1, 0)
        own_add(0)
        round_into(cg[1, 1][:, 0:512], last[2], nc.scalar.copy)
        quant_c(1, 1)
        own_add(1)
        copy_first(2)
        pool_max(2)
        hs = [fresh("h%d" % b, BF16) for b in range(4)]
        nc.scalar.activation(hs[0], sums[0], RELU)
        relu(1, hs[1])
        for b in range(2):
            hq[b] = quantise(hs[b], JB, "h%d" % b)
        own.append(bank([P, 4, JB], "own2", 1))
        for a in range(2):
            own_pass(nb[0, 3], 3, a, False, a == 1)
            own_pass(own[2], 2, a, a == 0, a == 1)
            own_pass(nb[1, 3], 3, a, False, a == 1)
        wdg = tile([P, 4 * N], BF16, "wdg")
        round_into(wdg[:], wd_raw, nc.scalar.copy)
        wd_codes, wd_sc = quantise(wdg[:], N, "wd")
        ys = {b: second(b, n) for b, n in ((0, 5), (1, 3))}
        own_add(2)
        clipped = runs(rows(wd_raw, 0, 2))
        nc.scalar.activation(clipped, woven(nb[0, 3]), RELU)
        nc.vector.tensor_tensor(runs(hs[3]), woven(nb[1, 3]), clipped, ALU.max)
        nc.scalar.activation(hs[2], sums[2], RELU)
        finish(0, ys[0], slice(0, 2))
        for b, n in ((3, 6), (2, 7)):
            hq[b] = quantise(hs[b], JB, "h%d" % b)
            ys[b] = second(b, n)
        for b in (1, 3):
            finish(b, ys[b], slice(0, 2))
        for nh in range(2):
            finish(2, ys[2], slice(nh, nh + 1))
